import numpy as np
import ml_dtypes


def mxq(x, axis, fmt="e4m3"):
    dtype, down = {"e4m3": (ml_dtypes.float8_e4m3fn, 7), "e5m2": (ml_dtypes.float8_e5m2, 14)}[fmt]
    v = np.moveaxis(np.asarray(x, np.float32).astype(ml_dtypes.bfloat16).astype(np.float64), axis, -1)
    blocks = v.reshape(v.shape[:-1] + (-1, 32))
    amax = np.abs(blocks).max(-1, keepdims=True)
    byte = np.maximum(np.where(amax > 0, np.frexp(amax)[1] - 1 + 127, 0) - down, 1)
    scale = np.exp2(byte - 127.0)
    codes = (blocks / scale).astype(np.float32).astype(dtype).astype(np.float64)
    return np.moveaxis((codes * scale).reshape(v.shape), -1, axis)


WIDE = False


def mx_kscale(k):
    if not WIDE:
        return np.ones(k)
    levels = np.array([10, -10, 5, -5, 0])
    if k % 512:
        return np.exp2(np.random.permutation(np.resize(levels, k // 32))).repeat(32)
    a = np.empty((k // 512, 16))
    for p in range(k // 512):
        a[p, :8] = np.random.permutation(np.resize(levels, 8))
        for g in range(8):
            far = levels[np.abs(levels - a[p, g]) >= 10]
            a[p, g + 8] = far[np.random.randint(len(far))]
    return np.exp2(a.ravel()).repeat(32)


BF16 = ml_dtypes.bfloat16


def bf(x):
    return np.asarray(x, np.float32).astype(BF16)


def f64(x):
    return np.asarray(x).astype(np.float64)


B, D, H, N, T = 1024, 1024, 512, 1024, 3


def sigmoid(v):
    return 1.0 / (1.0 + np.exp(-v))


def draw0():
    s, t = mx_kscale(D), mx_kscale(H)
    return {"x": bf(np.random.standard_normal((B, D)) * s),
            "w": bf(np.random.standard_normal((D, H)) / np.sqrt(D) / s[:, None]),
            "g": bf((1.0 + 0.1 * np.random.standard_normal(H)) * t),
            "wh": bf(np.random.standard_normal((T, H, N)) * 1.5 / np.sqrt(H) / t[None, :, None]),
            "o": bf(np.random.uniform(0.0, 1.0, (B, N))),
            "y": bf(np.random.uniform(0.0, 1.0, (B, N)))}


def shared_trunk(x, w, g):
    return f64(g)[None, :] * np.tanh(mxq(f64(x), 1, "e4m3") @ mxq(f64(w), 0, "e4m3"))


def core(x, w, g, wh, o, y):
    h = shared_trunk(x, w, g)
    z = mxq(h, 1, "e4m3") @ mxq(f64(wh), 1, "e4m3")
    p = np.maximum(sigmoid(z[0]), 0.2)
    err = np.square(f64(y) - sigmoid(z[1]))
    e = z[2]
    return e + f64(o) * (err - e) / p


def e4m3fn_bytes(y):
    return np.clip(np.asarray(y, np.float64), -448.0, 448.0).astype(np.float32).astype(ml_dtypes.float8_e4m3fn).view(np.uint8)


def e4m3fn_values(b):
    return np.asarray(b, np.uint8).view(ml_dtypes.float8_e4m3fn).astype(np.float64)


def setup_inputs():
    d = draw0()
    x0 = np.asarray(d['wh']).astype(np.float64)
    s = (np.max(np.abs(x0), axis=(0, 2), keepdims=True) / 448.0).astype(np.float32)
    out = {}
    for k, v in d.items():
        if k == 'wh':
            out['wh_bytes'] = e4m3fn_bytes(x0 / s.astype(np.float64))
            out['wh_scale'] = s
        else:
            out[k] = v
    return out


def reference(x, w, g, wh_bytes, wh_scale, o, y):
    return core(x, w, g, e4m3fn_values(wh_bytes) * wh_scale.astype(np.float64), o, y)

@@ -1,0 +1,330 @@
+from contextlib import ExitStack
+
+import concourse.mybir as mybir
+from concourse.masks import make_identity
+
+B, D, H, N, T = 1024, 1024, 512, 1024, 3
+FLOPS = 2 * B * D * H + 2 * T * B * H * N
+
+F32 = mybir.dt.float32
+BF16 = mybir.dt.bfloat16
+U32 = mybir.dt.uint32
+U8 = mybir.dt.uint8
+FP8X4 = mybir.dt.float8_e4m3fn_x4
+FP8 = mybir.dt.float8_e4m3fn
+ACT = mybir.ActivationFunctionType
+ALU = mybir.AluOpType
+
+P = 128
+BLOCKK = ('t', 'e', 'u', 'sq', 'r', 'f', 'w', 'wf', 'o', 'z0', 'z1', 'z2')
+NT = 512
+NB = B // P
+NH = N // NT
+
+U_PE = set(range(16))
+CLAMP_S = set([])
+W_G = set([0,1,2,3,4,5,6,7,8,9,10,11,12,13,14,15])
+WIDEN_V = set([(0, 0, 0), (0, 0, 1), (0, 0, 2), (0, 1, 0), (1, 0, 0), (1, 0, 1), (1, 1, 0), (1, 1, 1), (2, 0, 0), (2, 1, 0), (2, 1, 1)])
+IL_S = set([(0, 1), (1, 0)])
+G_GAIN = []
+IL_PE = set([])
+GSPLIT = 1
+CLAMP_G = set([])
+
+
+def tile_escmdoublyrobusterrormap_kernel(tc, x, w, g, wh_bytes, wh_scale, o, y, out):
+    nc = tc.nc
+    with ExitStack() as ctx:
+        const = ctx.enter_context(tc.tile_pool(name="const", bufs=1))
+        work = ctx.enter_context(tc.tile_pool(name="work", bufs=3))
+        psum = ctx.enter_context(tc.psum_pool(name="psum", bufs=1))
+        ctx.enter_context(tc.manual_schedule())
+
+        warm = const.tile([P, 1], F32)
+        nc.vector.memset(warm[:], 0.0)
+        nc.scalar.activation(out=warm[:], in_=warm[:], func=ACT.Exp)
+
+        s_sb = const.tile([P, 4], F32)
+        nc.scalar.dma_start(out=s_sb[:], in_=wh_scale.rearrange("o (p t) q -> p (o t q)", t=4))
+        g_bf = const.tile([P, 4], BF16)
+        nc.scalar.dma_start(out=g_bf[:], in_=g.rearrange("(p t) -> p t", t=4))
+
+        w_raw = {}
+        wh_b = {}
+        x_sb = {}
+        o_sb = {}
+        y_sb = {}
+
+        def load_w(c):
+            w_raw[c] = const.tile([P, 4, H], BF16, name="w_raw%d" % c)
+            nc.sync.dma_start(out=w_raw[c][:], in_=w[512 * c:512 * (c + 1), :].rearrange("(p j) c -> p j c", j=4))
+
+        def load_wh(t, h):
+            if t not in wh_b:
+                wh_b[t] = const.tile([P, 4, N], U8, name="wh_b%d" % t)
+            c = slice(NT * h, NT * (h + 1))
+            nc.sync.dma_start(out=wh_b[t][:, :, c], in_=wh_bytes[t, :, c].rearrange("(p j) n -> p j n", j=4))
+
+        def load_x(q):
+            x_sb[q] = const.tile([P, 2, D], BF16, name="x_sb%d" % q)
+            nc.sync.dma_start(out=x_sb[q][:], in_=x[256 * q:256 * (q + 1), :].rearrange("(i p) k -> p i k", p=P))
+
+        def load_oy(d, src, label, q):
+            d[q] = const.tile([P, 2, N], BF16, name="%s_%d" % (label, q))
+            nc.sync.dma_start(out=d[q][:], in_=src[256 * q:256 * (q + 1), :].rearrange("(i p) n -> p i n", p=P))
+
+        load_wh(1, 0)
+        load_wh(0, 0)
+        load_w(0)
+        load_x(0)
+        load_w(1)
+        load_wh(2, 1)
+        load_wh(2, 0)
+        load_wh(0, 1)
+        load_wh(1, 1)
+        load_oy(y_sb, y, "y", 0)
+        load_oy(o_sb, o, "o", 0)
+        load_x(2)
+        load_x(3)
+        load_x(1)
+        load_oy(y_sb, y, "y", 1)
+        load_oy(o_sb, o, "o", 1)
+        load_oy(y_sb, y, "y", 2)
+        load_oy(o_sb, o, "o", 2)
+        load_oy(y_sb, y, "y", 3)
+        load_oy(o_sb, o, "o", 3)
+
+        ident = const.tile([P, P], F32)
+        make_identity(nc, ident[:])
+        neg2 = const.tile([P, P], BF16)
+        if U_PE:
+            nc.gpsimd.tensor_scalar(out=neg2[:], in0=ident[:], scalar1=-2.0, scalar2=0.0, op0=ALU.mult, op1=ALU.add)
+        g_sb = const.tile([P, 4], F32)
+        nc.gpsimd.tensor_copy(out=g_sb[:], in_=g_bf[:])
+
+        w_g = {}
+        w_q = const.tile([P, 2, H], U32, align_bytes=64)
+        w_s = const.tile([P, 2, H], U8, align_bytes=64)
+        x_g = {}
+        x_q = const.tile([P, NB, 2, P], U32, align_bytes=64)
+        x_s = const.tile([P, NB, 2, P], U8, align_bytes=64)
+        wh_p = {}
+        wh_g = {}
+        wh_q = const.tile([P, T, N], U32, align_bytes=64)
+        wh_s = const.tile([P, T, N], U8, align_bytes=64)
+        h_q = const.tile([P, NB, P], U32, align_bytes=64)
+        h_s = const.tile([P, NB, P], U8, align_bytes=64)
+        xt = {}
+        ht = {}
+        th = {}
+        hg = {}
+
+        def w_inter(c):
+            w_g[c] = const.tile([P, 4 * H], BF16, name="w_g%d" % c, align_bytes=64)
+            nc.vector.tensor_copy(
+                out=w_g[c][:].rearrange("p (t m j) -> p t m j", t=4, j=4),
+                in_=w_raw[c][:].rearrange("p j (m t) -> p t m j", t=4),
+            )
+
+        def w_quant(c):
+            nc.vector.quantize_mx(out=w_q[:, c, :].bitcast(FP8X4), scales=w_s[:, c, :], in_=w_g[c][:])
+
+        def x_trans(i):
+            xt[i] = psum.tile([P, 2, 2, P], F32, name="xt", tag="aux", bufs=2)
+            words = x_sb[i // 2][:, i % 2, :].bitcast(F32)
+            for c in range(2):
+                for u in range(2):
+                    nc.tensor.transpose(xt[i][:, c, u, :], words[:, 256 * c + u:256 * (c + 1):2], ident[:])
+
+        def x_copy(i):
+            x_g[i] = work.tile([P, 2 * P * 4], BF16, name="x_g", align_bytes=64)
+            nc.scalar.copy(
+                out=x_g[i][:].bitcast(F32).rearrange("p (c r u) -> p c r u", c=2, u=2),
+                in_=xt[i][:].rearrange("p c u r -> p c r u"),
+            )
+
+        def x_quant(i):
+            nc.vector.quantize_mx(
+                out=x_q[:, i, :, :].rearrange("p c r -> p (c r)").bitcast(FP8X4),
+                scales=x_s[:, i, :, :].rearrange("p c r -> p (c r)"),
+                in_=x_g[i][:],
+            )
+
+        def h_matmul(i):
+            ht[i] = psum.tile([P, 4, P], F32, name="ht", tag="aux", bufs=2)
+            for t in range(4):
+                for c in range(2):
+                    nc.tensor.matmul_mx(
+                        out=ht[i][:, t, :],
+                        lhsT=w_q[:, c, P * t:P * (t + 1)].bitcast(FP8X4),
+                        lhsT_scale=w_s[:, c, P * t:P * (t + 1)],
+                        rhs=x_q[:, i, c, :].bitcast(FP8X4),
+                        rhs_scale=x_s[:, i, c, :],
+                        start=(c == 0),
+                        stop=(c == 1),
+                    )
+
+        def h_tanh(i):
+            th[i] = work.tile([P, P, 4], F32, name="th")
+            nc.scalar.activation(out=th[i][:], in_=ht[i][:].rearrange("p t n -> p n t"), func=ACT.Tanh)
+
+        def h_gain(i):
+            hg[i] = work.tile([P, P, 4], BF16, name="hg", align_bytes=64)
+            nc.vector.tensor_tensor(out=hg[i][:], in0=th[i][:], in1=g_sb[:].unsqueeze(1).to_broadcast([P, P, 4]), op=ALU.mult)
+
+        def h_quant(i):
+            nc.vector.quantize_mx(
+                out=h_q[:, i, :].bitcast(FP8X4), scales=h_s[:, i, :], in_=hg[i][:].rearrange("p n t -> p (n t)")
+            )
+
+        def wh_widen(t, h, j):
+            if (t, h) not in wh_p:
+                wh_p[t, h] = work.tile([P, 4, NT], BF16, name="wh_p", bufs=4)
+            if (t, h, j) in WIDEN_V:
+                nc.vector.tensor_scalar(
+                    out=wh_p[t, h][:, j, :], in0=wh_b[t][:, j, NT * h:NT * (h + 1)].bitcast(FP8), scalar1=s_sb[:, j:j + 1], scalar2=None, op0=ALU.mult)
+            else:
+                nc.scalar.activation(
+                    out=wh_p[t, h][:, j, :],
+                    in_=wh_b[t][:, j, NT * h:NT * (h + 1)].bitcast(FP8),
+                    func=ACT.Copy,
+                    scale=s_sb[:, j:j + 1],
+                )
+
+        def wh_inter(t, h):
+            wh_g[t, h] = work.tile([P, NT, 4], BF16, name="wh_g", align_bytes=64, bufs=4)
+            if (t, h) in IL_S:
+                nc.scalar.copy(out=wh_g[t, h][:], in_=wh_p[t, h][:].rearrange("p j n -> p n j"))
+            else:
+                nc.vector.tensor_copy(out=wh_g[t, h][:].rearrange("p (c i) j -> p c j i", i=4), in_=wh_p[t, h][:].rearrange("p j (c i) -> p c j i", i=4))
+
+        def wh_quant(t, h):
+            nc.vector.quantize_mx(
+                out=wh_q[:, t, NT * h:NT * (h + 1)].bitcast(FP8X4),
+                scales=wh_s[:, t, NT * h:NT * (h + 1)],
+                in_=wh_g[t, h][:].rearrange("p n j -> p (n j)"),
+            )
+
+        z = {}
+        tt = {}
+        ee = {}
+        uu = {}
+        er = {}
+        ww = {}
+        ff = {}
+
+        def hi(s):
+            return s % 2, s // 2
+
+        def z_matmul(s, t):
+            h, i = hi(s)
+            if t == 1:
+                z1 = psum.tile([P, NT], F32, name="z1")
+                z[s, t] = z1
+            elif t == 0:
+                z0 = psum.tile([P, NT], F32, name="z0")
+                z[s, t] = z0
+            else:
+                z2 = psum.tile([P, NT], F32, name="z2", bufs=3)
+                z[s, t] = z2
+            if t == 1 and s in U_PE:
+                for c in range(4):
+                    cols = slice(NT * h + P * c, NT * h + P * (c + 1))
+                    nc.tensor.matmul_mx(
+                        out=z[s, t][:, P * c:P * (c + 1)],
+                        lhsT=wh_q[:, t, cols].bitcast(FP8X4),
+                        lhsT_scale=wh_s[:, t, cols],
+                        rhs=h_q[:, i, :].bitcast(FP8X4),
+                        rhs_scale=h_s[:, i, :],
+                        start=True,
+                        stop=True,
+                    )
+                return
+            nc.tensor.matmul_mx(
+                out=z[s, t][:],
+                lhsT=h_q[:, i, :].bitcast(FP8X4),
+                lhsT_scale=h_s[:, i, :],
+                rhs=wh_q[:, t, NT * h:NT * (h + 1)].bitcast(FP8X4),
+                rhs_scale=wh_s[:, t, NT * h:NT * (h + 1)],
+                start=True,
+                stop=True,
+            )
+
+        def b_tanh(s):
+            tt[s] = work.tile([P, NT], F32, name="tt")
+            nc.scalar.activation(out=tt[s][:], in_=z[s, 1][:], func=ACT.Tanh, scale=0.5)
+
+        def b_exp(s):
+            ee[s] = work.tile([P, NT], F32, name="ee", bufs=4)
+            nc.scalar.activation(out=ee[s][:], in_=z[s, 0][:], func=ACT.Exp, scale=-1.0)
+
+        def b_u(s):
+            h, i = hi(s)
+            ysl = y_sb[i // 2][:, i % 2, NT * h:NT * (h + 1)]
+            if s in U_PE:
+                uu[s] = psum.tile([P, NT], F32, name="up", bufs=1)
+                nc.tensor.matmul(out=uu[s][:], lhsT=neg2[:], rhs=ysl, start=True, stop=False)
+                for c in range(4):
+                    cols = slice(P * c, P * (c + 1))
+                    nc.tensor.matmul(out=uu[s][:, cols], lhsT=tt[s][:, cols], rhs=ident[:], is_transpose=True, start=False, stop=(c == 3))
+            else:
+                uu[s] = work.tile([P, NT], F32, name="us")
+                nc.vector.scalar_tensor_tensor(out=uu[s][:], in0=ysl, scalar=-2.0, in1=tt[s][:], op0=ALU.mult, op1=ALU.add)
+
+        def b_sq(s):
+            er[s] = work.tile([P, NT], F32, name="er", bufs=4)
+            nc.scalar.activation(out=er[s][:], in_=uu[s][:], func=ACT.Square, scale=0.5, bias=0.5)
+
+        def b_clamp(s):
+            if s in CLAMP_S:
+                nc.scalar.activation(out=ee[s][:], in_=ee[s][:], func=ACT.Relu, scale=-1.0, bias=4.0)
+            else:
+                (nc.gpsimd if s in CLAMP_G else nc.vector).tensor_scalar(out=ee[s][:], in0=ee[s][:], scalar1=4.0, scalar2=1.0, op0=ALU.min, op1=ALU.add)
+
+        def b_w(s):
+            h, i = hi(s)
+            osl = o_sb[i // 2][:, i % 2, NT * h:NT * (h + 1)]
+            ww[s] = work.tile([P, NT], F32, name="ww", bufs=4)
+            if s in CLAMP_S:
+                nc.vector.scalar_tensor_tensor(out=ww[s][:], in0=ee[s][:], scalar=5.0, in1=osl, op0=ALU.subtract, op1=ALU.mult)
+            elif s in W_G:
+                for q in range(GSPLIT):
+                    c = slice(NT // GSPLIT * q, NT // GSPLIT * (q + 1))
+                    nc.gpsimd.tensor_tensor(out=ww[s][:, c], in0=ee[s][:, c], in1=osl[:, c], op=ALU.mult)
+            else:
+                nc.vector.tensor_tensor(out=ww[s][:], in0=ee[s][:], in1=osl, op=ALU.mult)
+
+        def b_f(s):
+            ff[s] = work.tile([P, NT], F32, name="ff")
+            if s in CLAMP_S:
+                nc.vector.tensor_tensor(out=ff[s][:], in0=z[s, 2][:], in1=er[s][:], op=ALU.subtract)
+            else:
+                nc.vector.tensor_tensor(out=ff[s][:], in0=er[s][:], in1=z[s, 2][:], op=ALU.subtract)
+
+        def b_wf(s):
+            nc.vector.tensor_tensor(out=ff[s][:], in0=ww[s][:], in1=ff[s][:], op=ALU.mult)
+
+        def b_out(s):
+            h, i = hi(s)
+            ot = work.tile([P, NT], F32, name="ot", bufs=4)
+            nc.vector.tensor_tensor(out=ot[:], in0=z[s, 2][:], in1=ff[s][:], op=ALU.add)
+            nc.sync.dma_start(out=out[P * i:P * (i + 1), NT * h:NT * (h + 1)], in_=ot[:])
+
+        calls = {
+            "wid": wh_widen, "il": wh_inter, "q": wh_quant, "wil": w_inter, "wq": w_quant, "X": x_trans, "Xc": x_copy, "Xq": x_quant,
+            "H": h_matmul, "Ht": h_tanh, "G": h_gain, "Q": h_quant, "t": b_tanh, "e": b_exp, "u": b_u, "sq": b_sq,
+            "r": b_clamp, "f": b_f, "w": b_w, "wf": b_wf, "o": b_out,
+            "z0": lambda s: z_matmul(s, 0), "z1": lambda s: z_matmul(s, 1), "z2": lambda s: z_matmul(s, 2),
+        }
+        HEAD = [("wid", 1, 0, 1), ("wid", 1, 0, 0), ("wid", 0, 0, 2), ("X", 1), ("X", 0), ("wid", 0, 0, 0), ("wid", 1, 0, 3), ("wid", 0, 0, 3), ("wid", 1, 0, 2), ("il", 1, 0), ("Xc", 1), ("wid", 0, 0, 1), ("wil", 0), ("Xc", 0), ("wid", 2, 0, 2), ("il", 0, 0), ("wil", 1), ("wid", 1, 1, 3), ("wq", 0), ("wid", 0, 1, 0), ("wq", 1), ("Xq", 1), ("wid", 1, 1, 0), ("Xq", 0), ("wid", 2, 0, 1), ("wid", 1, 1, 1), ("wid", 2, 0, 3), ("wid", 2, 1, 0), ("q", 0, 0), ("H", 1), ("wid", 0, 1, 2), ("wid", 2, 1, 2), ("H", 0), ("wid", 2, 1, 3), ("wid", 2, 1, 1), ("wid", 2, 0, 0), ("wid", 0, 1, 1), ("il", 2, 1), ("Ht", 0), ("wid", 1, 1, 2), ("wid", 0, 1, 3), ("Ht", 1), ("X", 3), ("X", 2), ("q", 1, 0), ("G", 0), ("il", 1, 1), ("Q", 0), ("il", 2, 0), ("q", 1, 1), ("q", 2, 0), ("q", 2, 1), ("il", 0, 1), ("z0", 0), ("Xc", 3), ("Xc", 2), ("z1", 0), ("q", 0, 1), ("Xq", 2), ("Xq", 3)]
+        SLOT = [("z2", 0, 1), ("Xq", 4, 0), ("G", 2, 0), ("w", 0, 0), ("w", 0, 1), ("t", 1, 0), ("f", 0, 0), ("f", 0, 1), ("e", 1, 0), ("X", 5, 0), ("z2", 1, 0), ("wf", 0, 0), ("z1", 1, 1), ("r", 1, 0), ("Xc", 5, 0), ("u", 1, 0), ("z0", 1, 1), ("Q", 2, 0), ("wf", 0, 1), ("t", 1, 1), ("H", 3, 0), ("sq", 1, 0), ("u", 1, 1), ("o", 0, 0), ("e", 1, 1), ("z1", 2, 0), ("Ht", 3, 0), ("o", 0, 1), ("sq", 1, 1), ("r", 1, 1), ("z0", 2, 0)]
+        done = set()
+        for task in HEAD:
+            calls[task[0]](*task[1:])
+            done.add(task)
+        for i in range(-1, NB + 1):
+            for k, d, h in SLOT:
+                task = (k, 2 * (i + d) + h) if k in BLOCKK else (k, i + d)
+                if 0 <= i + d < NB and task not in done:
+                    calls[k](*task[1:])
+                    done.add(task)

@@ -16,20 +16,15 @@ ACT = mybir.ActivationFunctionType
 ALU = mybir.AluOpType
 
 P = 128
-BLOCKK = ('t', 'e', 'u', 'sq', 'r', 'f', 'w', 'wf', 'o', 'z0', 'z1', 'z2')
 NT = 512
 NB = B // P
 NH = N // NT
-
-U_PE = set(range(16))
-CLAMP_S = set([])
-W_G = set([0,1,2,3,4,5,6,7,8,9,10,11,12,13,14,15])
-WIDEN_V = set([(0, 0, 0), (0, 0, 1), (0, 0, 2), (0, 1, 0), (1, 0, 0), (1, 0, 1), (1, 1, 0), (1, 1, 1), (2, 0, 0), (2, 1, 0), (2, 1, 1)])
-IL_S = set([(0, 1), (1, 0)])
-G_GAIN = []
-IL_PE = set([])
-GSPLIT = 1
-CLAMP_G = set([])
+Z2B = 3
+UB = 1
+AUXB = 1
+NV = 1
+NV2 = 2
+GCUT = 128
 
 
 def tile_escmdoublyrobusterrormap_kernel(tc, x, w, g, wh_bytes, wh_scale, o, y, out):
@@ -40,14 +35,13 @@ def tile_escmdoublyrobusterrormap_kernel(tc, x, w, g, wh_bytes, wh_scale, o, y, 
         psum = ctx.enter_context(tc.psum_pool(name="psum", bufs=1))
         ctx.enter_context(tc.manual_schedule())
 
-        warm = const.tile([P, 1], F32)
+        s_sb = const.tile([P, 4], F32, name="s_sb")
+        nc.scalar.dma_start(out=s_sb[:], in_=wh_scale.rearrange("o (p t) q -> p (o t q)", t=4))
+        g_bf = const.tile([P, 4], BF16, name="g_bf")
+        nc.scalar.dma_start(out=g_bf[:], in_=g.rearrange("(p t) -> p t", t=4))
+        warm = const.tile([P, 1], F32, name="warm")
         nc.vector.memset(warm[:], 0.0)
         nc.scalar.activation(out=warm[:], in_=warm[:], func=ACT.Exp)
-
-        s_sb = const.tile([P, 4], F32)
-        nc.scalar.dma_start(out=s_sb[:], in_=wh_scale.rearrange("o (p t) q -> p (o t q)", t=4))
-        g_bf = const.tile([P, 4], BF16)
-        nc.scalar.dma_start(out=g_bf[:], in_=g.rearrange("(p t) -> p t", t=4))
 
         w_raw = {}
         wh_b = {}
@@ -59,68 +53,58 @@ def tile_escmdoublyrobusterrormap_kernel(tc, x, w, g, wh_bytes, wh_scale, o, y, 
             w_raw[c] = const.tile([P, 4, H], BF16, name="w_raw%d" % c)
             nc.sync.dma_start(out=w_raw[c][:], in_=w[512 * c:512 * (c + 1), :].rearrange("(p j) c -> p j c", j=4))
 
-        def load_wh(t, h):
-            if t not in wh_b:
-                wh_b[t] = const.tile([P, 4, N], U8, name="wh_b%d" % t)
-            c = slice(NT * h, NT * (h + 1))
-            nc.sync.dma_start(out=wh_b[t][:, :, c], in_=wh_bytes[t, :, c].rearrange("(p j) n -> p j n", j=4))
+        def load_wh(t, parts=1):
+            wh_b[t] = const.tile([P, 4, N], U8, name="wh_b%d" % t)
+            src = wh_bytes[t].rearrange("(p j) n -> p j n", j=4)
+            for j0 in range(0, 4, 4 // parts):
+                nc.sync.dma_start(out=wh_b[t][:, j0:j0 + 4 // parts, :], in_=src[:, j0:j0 + 4 // parts, :])
 
-        def load_x(q):
-            x_sb[q] = const.tile([P, 2, D], BF16, name="x_sb%d" % q)
-            nc.sync.dma_start(out=x_sb[q][:], in_=x[256 * q:256 * (q + 1), :].rearrange("(i p) k -> p i k", p=P))
+        def load_rows(d, src, label, i):
+            d[i] = const.tile([P, N], BF16, name="%s_%d" % (label, i))
+            nc.sync.dma_start(out=d[i][:], in_=src[P * i:P * (i + 1), :])
 
-        def load_oy(d, src, label, q):
-            d[q] = const.tile([P, 2, N], BF16, name="%s_%d" % (label, q))
-            nc.sync.dma_start(out=d[q][:], in_=src[256 * q:256 * (q + 1), :].rearrange("(i p) n -> p i n", p=P))
-
-        load_wh(1, 0)
-        load_wh(0, 0)
+        load_wh(0, 2)
         load_w(0)
-        load_x(0)
+        load_rows(x_sb, x, "x", 0)
+        load_wh(1)
         load_w(1)
-        load_wh(2, 1)
-        load_wh(2, 0)
-        load_wh(0, 1)
-        load_wh(1, 1)
-        load_oy(y_sb, y, "y", 0)
-        load_oy(o_sb, o, "o", 0)
-        load_x(2)
-        load_x(3)
-        load_x(1)
-        load_oy(y_sb, y, "y", 1)
-        load_oy(o_sb, o, "o", 1)
-        load_oy(y_sb, y, "y", 2)
-        load_oy(o_sb, o, "o", 2)
-        load_oy(y_sb, y, "y", 3)
-        load_oy(o_sb, o, "o", 3)
+        load_rows(x_sb, x, "x", 1)
+        load_wh(2)
+        load_rows(x_sb, x, "x", 2)
+        load_rows(x_sb, x, "x", 3)
+        for i in range(NB):
+            load_rows(y_sb, y, "y", i)
+            load_rows(o_sb, o, "o", i)
+            if i + 4 < NB:
+                load_rows(x_sb, x, "x", i + 4)
 
-        ident = const.tile([P, P], F32)
+        ident = const.tile([P, P], F32, name="ident")
         make_identity(nc, ident[:])
-        neg2 = const.tile([P, P], BF16)
-        if U_PE:
-            nc.gpsimd.tensor_scalar(out=neg2[:], in0=ident[:], scalar1=-2.0, scalar2=0.0, op0=ALU.mult, op1=ALU.add)
-        g_sb = const.tile([P, 4], F32)
-        nc.gpsimd.tensor_copy(out=g_sb[:], in_=g_bf[:])
+        neg2 = const.tile([P, P], BF16, name="neg2")
+        nc.gpsimd.tensor_scalar(out=neg2[:], in0=ident[:], scalar1=-2.0, scalar2=0.0, op0=ALU.mult, op1=ALU.add)
+        ident_bf = const.tile([P, P], BF16, name="ident_bf")
+        nc.gpsimd.tensor_scalar(out=ident_bf[:], in0=ident[:], scalar1=1.0, scalar2=0.0, op0=ALU.mult, op1=ALU.add)
+        g_ps = psum.tile([P, 4], F32, name="g_ps")
 
         w_g = {}
-        w_q = const.tile([P, 2, H], U32, align_bytes=64)
-        w_s = const.tile([P, 2, H], U8, align_bytes=64)
+        w_q = const.tile([P, 2, H], U32, align_bytes=64, name="w_q")
+        w_s = const.tile([P, 2, H], U8, align_bytes=64, name="w_s")
         x_g = {}
-        x_q = const.tile([P, NB, 2, P], U32, align_bytes=64)
-        x_s = const.tile([P, NB, 2, P], U8, align_bytes=64)
+        x_q = const.tile([P, NB, 2, P], U32, align_bytes=64, name="x_q")
+        x_s = const.tile([P, NB, 2, P], U8, align_bytes=64, name="x_s")
         wh_p = {}
         wh_g = {}
-        wh_q = const.tile([P, T, N], U32, align_bytes=64)
-        wh_s = const.tile([P, T, N], U8, align_bytes=64)
-        h_q = const.tile([P, NB, P], U32, align_bytes=64)
-        h_s = const.tile([P, NB, P], U8, align_bytes=64)
+        wh_q = const.tile([P, T, N], U32, align_bytes=64, name="wh_q")
+        wh_s = const.tile([P, T, N], U8, align_bytes=64, name="wh_s")
+        h_q = const.tile([P, NB, P], U32, align_bytes=64, name="h_q")
+        h_s = const.tile([P, NB, P], U8, align_bytes=64, name="h_s")
         xt = {}
         ht = {}
         th = {}
         hg = {}
 
         def w_inter(c):
-            w_g[c] = const.tile([P, 4 * H], BF16, name="w_g%d" % c, align_bytes=64)
+            w_g[c] = work.tile([P, 4 * H], BF16, name="w_g", align_bytes=64, bufs=2)
             nc.vector.tensor_copy(
                 out=w_g[c][:].rearrange("p (t m j) -> p t m j", t=4, j=4),
                 in_=w_raw[c][:].rearrange("p j (m t) -> p t m j", t=4),
@@ -130,13 +114,17 @@ def tile_escmdoublyrobusterrormap_kernel(tc, x, w, g, wh_bytes, wh_scale, o, y, 
             nc.vector.quantize_mx(out=w_q[:, c, :].bitcast(FP8X4), scales=w_s[:, c, :], in_=w_g[c][:])
 
         def x_trans(i):
-            xt[i] = psum.tile([P, 2, 2, P], F32, name="xt", tag="aux", bufs=2)
-            words = x_sb[i // 2][:, i % 2, :].bitcast(F32)
+            if i >= NB:
+                return
+            xt[i] = psum.tile([P, 2, 2, P], F32, name="xt", tag="z2" if i < 3 else "aux", bufs=Z2B if i < 3 else AUXB)
+            words = x_sb[i][:].bitcast(F32)
             for c in range(2):
                 for u in range(2):
                     nc.tensor.transpose(xt[i][:, c, u, :], words[:, 256 * c + u:256 * (c + 1):2], ident[:])
 
         def x_copy(i):
+            if i >= NB:
+                return
             x_g[i] = work.tile([P, 2 * P * 4], BF16, name="x_g", align_bytes=64)
             nc.scalar.copy(
                 out=x_g[i][:].bitcast(F32).rearrange("p (c r u) -> p c r u", c=2, u=2),
@@ -144,6 +132,8 @@ def tile_escmdoublyrobusterrormap_kernel(tc, x, w, g, wh_bytes, wh_scale, o, y, 
             )
 
         def x_quant(i):
+            if i >= NB:
+                return
             nc.vector.quantize_mx(
                 out=x_q[:, i, :, :].rearrange("p c r -> p (c r)").bitcast(FP8X4),
                 scales=x_s[:, i, :, :].rearrange("p c r -> p (c r)"),
@@ -151,7 +141,9 @@ def tile_escmdoublyrobusterrormap_kernel(tc, x, w, g, wh_bytes, wh_scale, o, y, 
             )
 
         def h_matmul(i):
-            ht[i] = psum.tile([P, 4, P], F32, name="ht", tag="aux", bufs=2)
+            if i >= NB:
+                return
+            ht[i] = psum.tile([P, 4, P], F32, name="ht", tag="up" if i == 1 else "aux", bufs=AUXB)
             for t in range(4):
                 for c in range(2):
                     nc.tensor.matmul_mx(
@@ -165,38 +157,36 @@ def tile_escmdoublyrobusterrormap_kernel(tc, x, w, g, wh_bytes, wh_scale, o, y, 
                     )
 
         def h_tanh(i):
+            if i >= NB:
+                return
             th[i] = work.tile([P, P, 4], F32, name="th")
             nc.scalar.activation(out=th[i][:], in_=ht[i][:].rearrange("p t n -> p n t"), func=ACT.Tanh)
 
         def h_gain(i):
+            if i >= NB:
+                return
             hg[i] = work.tile([P, P, 4], BF16, name="hg", align_bytes=64)
-            nc.vector.tensor_tensor(out=hg[i][:], in0=th[i][:], in1=g_sb[:].unsqueeze(1).to_broadcast([P, P, 4]), op=ALU.mult)
+            nc.vector.tensor_tensor(out=hg[i][:], in0=th[i][:], in1=g_ps[:].unsqueeze(1).to_broadcast([P, P, 4]), op=ALU.mult)
 
         def h_quant(i):
+            if i >= NB:
+                return
             nc.vector.quantize_mx(
                 out=h_q[:, i, :].bitcast(FP8X4), scales=h_s[:, i, :], in_=hg[i][:].rearrange("p n t -> p (n t)")
             )
 
-        def wh_widen(t, h, j):
+        def wh_widen(t, h, j, on_vector):
             if (t, h) not in wh_p:
                 wh_p[t, h] = work.tile([P, 4, NT], BF16, name="wh_p", bufs=4)
-            if (t, h, j) in WIDEN_V:
-                nc.vector.tensor_scalar(
-                    out=wh_p[t, h][:, j, :], in0=wh_b[t][:, j, NT * h:NT * (h + 1)].bitcast(FP8), scalar1=s_sb[:, j:j + 1], scalar2=None, op0=ALU.mult)
+            src = wh_b[t][:, j, NT * h:NT * (h + 1)].bitcast(FP8)
+            if on_vector:
+                nc.vector.tensor_scalar(out=wh_p[t, h][:, j, :], in0=src, scalar1=s_sb[:, j:j + 1], scalar2=None, op0=ALU.mult)
             else:
-                nc.scalar.activation(
-                    out=wh_p[t, h][:, j, :],
-                    in_=wh_b[t][:, j, NT * h:NT * (h + 1)].bitcast(FP8),
-                    func=ACT.Copy,
-                    scale=s_sb[:, j:j + 1],
-                )
+                nc.scalar.activation(out=wh_p[t, h][:, j, :], in_=src, func=ACT.Copy, scale=s_sb[:, j:j + 1])
 
         def wh_inter(t, h):
-            wh_g[t, h] = work.tile([P, NT, 4], BF16, name="wh_g", align_bytes=64, bufs=4)
-            if (t, h) in IL_S:
-                nc.scalar.copy(out=wh_g[t, h][:], in_=wh_p[t, h][:].rearrange("p j n -> p n j"))
-            else:
-                nc.vector.tensor_copy(out=wh_g[t, h][:].rearrange("p (c i) j -> p c j i", i=4), in_=wh_p[t, h][:].rearrange("p j (c i) -> p c j i", i=4))
+            wh_g[t, h] = work.tile([P, NT, 4], BF16, name="wh_g", align_bytes=64, bufs=3)
+            nc.vector.tensor_copy(out=wh_g[t, h][:].rearrange("p (c i) j -> p c j i", i=4), in_=wh_p[t, h][:].rearrange("p j (c i) -> p c j i", i=4))
 
         def wh_quant(t, h):
             nc.vector.quantize_mx(
@@ -213,25 +203,15 @@ def tile_escmdoublyrobusterrormap_kernel(tc, x, w, g, wh_bytes, wh_scale, o, y, 
         ww = {}
         ff = {}
 
-        def hi(s):
-            return s % 2, s // 2
-
-        def z_matmul(s, t):
-            h, i = hi(s)
+        def z_matmul(t, i, h):
+            if i >= NB:
+                return
+            z[t, i, h] = psum.tile([P, NT], F32, name="z%d" % t, bufs=Z2B if t == 2 else 1)
             if t == 1:
-                z1 = psum.tile([P, NT], F32, name="z1")
-                z[s, t] = z1
-            elif t == 0:
-                z0 = psum.tile([P, NT], F32, name="z0")
-                z[s, t] = z0
-            else:
-                z2 = psum.tile([P, NT], F32, name="z2", bufs=3)
-                z[s, t] = z2
-            if t == 1 and s in U_PE:
                 for c in range(4):
                     cols = slice(NT * h + P * c, NT * h + P * (c + 1))
                     nc.tensor.matmul_mx(
-                        out=z[s, t][:, P * c:P * (c + 1)],
+                        out=z[t, i, h][:, P * c:P * (c + 1)],
                         lhsT=wh_q[:, t, cols].bitcast(FP8X4),
                         lhsT_scale=wh_s[:, t, cols],
                         rhs=h_q[:, i, :].bitcast(FP8X4),
@@ -241,7 +221,7 @@ def tile_escmdoublyrobusterrormap_kernel(tc, x, w, g, wh_bytes, wh_scale, o, y, 
                     )
                 return
             nc.tensor.matmul_mx(
-                out=z[s, t][:],
+                out=z[t, i, h][:],
                 lhsT=h_q[:, i, :].bitcast(FP8X4),
                 lhsT_scale=h_s[:, i, :],
                 rhs=wh_q[:, t, NT * h:NT * (h + 1)].bitcast(FP8X4),
@@ -250,81 +230,170 @@ def tile_escmdoublyrobusterrormap_kernel(tc, x, w, g, wh_bytes, wh_scale, o, y, 
                 stop=True,
             )
 
-        def b_tanh(s):
-            tt[s] = work.tile([P, NT], F32, name="tt")
-            nc.scalar.activation(out=tt[s][:], in_=z[s, 1][:], func=ACT.Tanh, scale=0.5)
+        def b_tanh(i, h):
+            if i >= NB:
+                return
+            tt[i, h] = work.tile([P, NT], F32, name="tt")
+            nc.scalar.activation(out=tt[i, h][:], in_=z[1, i, h][:], func=ACT.Tanh, scale=0.5)
 
-        def b_exp(s):
-            ee[s] = work.tile([P, NT], F32, name="ee", bufs=4)
-            nc.scalar.activation(out=ee[s][:], in_=z[s, 0][:], func=ACT.Exp, scale=-1.0)
+        def b_exp(i, h):
+            if i >= NB:
+                return
+            if h == 0:
+                ee[i] = work.tile([P, N], F32, name="ee")
+            nc.scalar.activation(out=ee[i][:, NT * h:NT * (h + 1)], in_=z[0, i, h][:], func=ACT.Exp, scale=-1.0)
 
-        def b_u(s):
-            h, i = hi(s)
-            ysl = y_sb[i // 2][:, i % 2, NT * h:NT * (h + 1)]
-            if s in U_PE:
-                uu[s] = psum.tile([P, NT], F32, name="up", bufs=1)
-                nc.tensor.matmul(out=uu[s][:], lhsT=neg2[:], rhs=ysl, start=True, stop=False)
-                for c in range(4):
-                    cols = slice(P * c, P * (c + 1))
-                    nc.tensor.matmul(out=uu[s][:, cols], lhsT=tt[s][:, cols], rhs=ident[:], is_transpose=True, start=False, stop=(c == 3))
-            else:
-                uu[s] = work.tile([P, NT], F32, name="us")
-                nc.vector.scalar_tensor_tensor(out=uu[s][:], in0=ysl, scalar=-2.0, in1=tt[s][:], op0=ALU.mult, op1=ALU.add)
+        def b_u(i, h):
+            uu[i, h] = psum.tile([P, NT], F32, name="up", bufs=UB)
+            nc.tensor.matmul(out=uu[i, h][:], lhsT=neg2[:], rhs=y_sb[i][:, NT * h:NT * (h + 1)], start=True, stop=False)
+            for c in range(4):
+                cols = slice(P * c, P * (c + 1))
+                nc.tensor.matmul(out=uu[i, h][:, cols], lhsT=tt[i, h][:, cols], rhs=ident[:], is_transpose=True, start=False, stop=(c == 3))
 
-        def b_sq(s):
-            er[s] = work.tile([P, NT], F32, name="er", bufs=4)
-            nc.scalar.activation(out=er[s][:], in_=uu[s][:], func=ACT.Square, scale=0.5, bias=0.5)
+        def b_sq(i, h):
+            er[i, h] = work.tile([P, NT], F32, name="er", bufs=4)
+            nc.scalar.activation(out=er[i, h][:], in_=uu[i, h][:], func=ACT.Square, scale=0.5, bias=0.5)
 
-        def b_clamp(s):
-            if s in CLAMP_S:
-                nc.scalar.activation(out=ee[s][:], in_=ee[s][:], func=ACT.Relu, scale=-1.0, bias=4.0)
-            else:
-                (nc.gpsimd if s in CLAMP_G else nc.vector).tensor_scalar(out=ee[s][:], in0=ee[s][:], scalar1=4.0, scalar2=1.0, op0=ALU.min, op1=ALU.add)
+        def b_clamp(i):
+            nc.vector.tensor_scalar(out=ee[i][:], in0=ee[i][:], scalar1=4.0, scalar2=1.0, op0=ALU.min, op1=ALU.add)
 
-        def b_w(s):
-            h, i = hi(s)
-            osl = o_sb[i // 2][:, i % 2, NT * h:NT * (h + 1)]
-            ww[s] = work.tile([P, NT], F32, name="ww", bufs=4)
-            if s in CLAMP_S:
-                nc.vector.scalar_tensor_tensor(out=ww[s][:], in0=ee[s][:], scalar=5.0, in1=osl, op0=ALU.subtract, op1=ALU.mult)
-            elif s in W_G:
-                for q in range(GSPLIT):
-                    c = slice(NT // GSPLIT * q, NT // GSPLIT * (q + 1))
-                    nc.gpsimd.tensor_tensor(out=ww[s][:, c], in0=ee[s][:, c], in1=osl[:, c], op=ALU.mult)
-            else:
-                nc.vector.tensor_tensor(out=ww[s][:], in0=ee[s][:], in1=osl, op=ALU.mult)
+        def pool_share(i):
+            return N - GCUT * ((i == 0) * 2 + (i + 2 >= NB))
 
-        def b_f(s):
-            ff[s] = work.tile([P, NT], F32, name="ff")
-            if s in CLAMP_S:
-                nc.vector.tensor_tensor(out=ff[s][:], in0=z[s, 2][:], in1=er[s][:], op=ALU.subtract)
-            else:
-                nc.vector.tensor_tensor(out=ff[s][:], in0=er[s][:], in1=z[s, 2][:], op=ALU.subtract)
+        def b_w(i):
+            ww[i] = work.tile([P, N], F32, name="ww", bufs=2)
+            c = slice(0, pool_share(i))
+            nc.gpsimd.tensor_tensor(out=ww[i][:, c], in0=ee[i][:, c], in1=o_sb[i][:, c], op=ALU.mult)
 
-        def b_wf(s):
-            nc.vector.tensor_tensor(out=ff[s][:], in0=ww[s][:], in1=ff[s][:], op=ALU.mult)
+        def b_w_rest(i):
+            c = slice(pool_share(i), N)
+            if pool_share(i) < N:
+                nc.vector.tensor_tensor(out=ww[i][:, c], in0=ee[i][:, c], in1=o_sb[i][:, c], op=ALU.mult)
 
-        def b_out(s):
-            h, i = hi(s)
-            ot = work.tile([P, NT], F32, name="ot", bufs=4)
-            nc.vector.tensor_tensor(out=ot[:], in0=z[s, 2][:], in1=ff[s][:], op=ALU.add)
-            nc.sync.dma_start(out=out[P * i:P * (i + 1), NT * h:NT * (h + 1)], in_=ot[:])
+        def b_f(i, h):
+            if h == 0:
+                ff[i] = work.tile([P, N], F32, name="ff", bufs=2)
+            nc.vector.tensor_tensor(out=ff[i][:, NT * h:NT * (h + 1)], in0=er[i, h][:], in1=z[2, i, h][:], op=ALU.subtract)
 
-        calls = {
-            "wid": wh_widen, "il": wh_inter, "q": wh_quant, "wil": w_inter, "wq": w_quant, "X": x_trans, "Xc": x_copy, "Xq": x_quant,
-            "H": h_matmul, "Ht": h_tanh, "G": h_gain, "Q": h_quant, "t": b_tanh, "e": b_exp, "u": b_u, "sq": b_sq,
-            "r": b_clamp, "f": b_f, "w": b_w, "wf": b_wf, "o": b_out,
-            "z0": lambda s: z_matmul(s, 0), "z1": lambda s: z_matmul(s, 1), "z2": lambda s: z_matmul(s, 2),
-        }
-        HEAD = [("wid", 1, 0, 1), ("wid", 1, 0, 0), ("wid", 0, 0, 2), ("X", 1), ("X", 0), ("wid", 0, 0, 0), ("wid", 1, 0, 3), ("wid", 0, 0, 3), ("wid", 1, 0, 2), ("il", 1, 0), ("Xc", 1), ("wid", 0, 0, 1), ("wil", 0), ("Xc", 0), ("wid", 2, 0, 2), ("il", 0, 0), ("wil", 1), ("wid", 1, 1, 3), ("wq", 0), ("wid", 0, 1, 0), ("wq", 1), ("Xq", 1), ("wid", 1, 1, 0), ("Xq", 0), ("wid", 2, 0, 1), ("wid", 1, 1, 1), ("wid", 2, 0, 3), ("wid", 2, 1, 0), ("q", 0, 0), ("H", 1), ("wid", 0, 1, 2), ("wid", 2, 1, 2), ("H", 0), ("wid", 2, 1, 3), ("wid", 2, 1, 1), ("wid", 2, 0, 0), ("wid", 0, 1, 1), ("il", 2, 1), ("Ht", 0), ("wid", 1, 1, 2), ("wid", 0, 1, 3), ("Ht", 1), ("X", 3), ("X", 2), ("q", 1, 0), ("G", 0), ("il", 1, 1), ("Q", 0), ("il", 2, 0), ("q", 1, 1), ("q", 2, 0), ("q", 2, 1), ("il", 0, 1), ("z0", 0), ("Xc", 3), ("Xc", 2), ("z1", 0), ("q", 0, 1), ("Xq", 2), ("Xq", 3)]
-        SLOT = [("z2", 0, 1), ("Xq", 4, 0), ("G", 2, 0), ("w", 0, 0), ("w", 0, 1), ("t", 1, 0), ("f", 0, 0), ("f", 0, 1), ("e", 1, 0), ("X", 5, 0), ("z2", 1, 0), ("wf", 0, 0), ("z1", 1, 1), ("r", 1, 0), ("Xc", 5, 0), ("u", 1, 0), ("z0", 1, 1), ("Q", 2, 0), ("wf", 0, 1), ("t", 1, 1), ("H", 3, 0), ("sq", 1, 0), ("u", 1, 1), ("o", 0, 0), ("e", 1, 1), ("z1", 2, 0), ("Ht", 3, 0), ("o", 0, 1), ("sq", 1, 1), ("r", 1, 1), ("z0", 2, 0)]
-        done = set()
-        for task in HEAD:
-            calls[task[0]](*task[1:])
-            done.add(task)
-        for i in range(-1, NB + 1):
-            for k, d, h in SLOT:
-                task = (k, 2 * (i + d) + h) if k in BLOCKK else (k, i + d)
-                if 0 <= i + d < NB and task not in done:
-                    calls[k](*task[1:])
-                    done.add(task)
+        def b_wf(i, cols):
+            nc.vector.tensor_tensor(out=ff[i][:, cols], in0=ww[i][:, cols], in1=ff[i][:, cols], op=ALU.mult)
+
+        def b_out(i, c0, width):
+            h = c0 // NT
+            ot = work.tile([P, width], F32, name="ot", bufs=4)
+            nc.vector.tensor_tensor(out=ot[:], in0=z[2, i, h][:, c0 - NT * h:c0 - NT * h + width], in1=ff[i][:, c0:c0 + width], op=ALU.add)
+            nc.sync.dma_start(out=out[P * i:P * (i + 1), c0:c0 + width], in_=ot[:])
+
+
+        def widen(t, h, planes=range(4), on_vector=False):
+            for j in planes:
+                wh_widen(t, h, j, on_vector)
+
+        wh_widen(0, 0, 0, True)
+        wh_widen(0, 0, 1, False)
+        wh_widen(0, 1, 0, True)
+        wh_widen(0, 1, 1, False)
+        wh_widen(0, 0, 2, True)
+        wh_widen(0, 0, 3, False)
+        wh_widen(0, 1, 2, True)
+        wh_widen(0, 1, 3, False)
+        x_trans(0)
+        nc.tensor.matmul(out=g_ps[:], lhsT=ident_bf[:], rhs=g_bf[:], start=True, stop=True)
+        x_trans(1)
+        w_inter(0)
+        x_copy(0)
+        wh_inter(0, 0)
+        w_quant(0)
+        widen(1, 0)
+        w_inter(1)
+        x_trans(2)
+        x_quant(0)
+        w_quant(1)
+        h_matmul(0)
+        x_copy(1)
+        widen(1, 1)
+        wh_inter(0, 1)
+        x_quant(1)
+        h_matmul(1)
+        wh_quant(0, 0)
+        h_tanh(0)
+        x_copy(2)
+        wh_inter(1, 0)
+        h_gain(0)
+        widen(2, 0, range(4 - NV), False)
+        wh_quant(1, 0)
+        h_quant(0)
+        x_quant(2)
+        wh_inter(1, 1)
+        wh_quant(0, 1)
+        h_tanh(1)
+        z_matmul(0, 0, 0)
+        z_matmul(1, 0, 0)
+        wh_quant(1, 1)
+        widen(2, 0, range(4 - NV, 4), True)
+
+        for k in range(NB):
+            b_exp(k, 0)
+            x_trans(k + 3)
+            if k == 1:
+                wh_quant(2, 1)
+                z_matmul(2, 0, 1)
+            if k > 0:
+                b_clamp(k - 1)
+                b_w(k - 1)
+            if k > 1:
+                b_out(k - 2, 0, NT)
+            b_tanh(k, 0)
+            if k > 1:
+                z_matmul(2, k - 1, 1)
+            z_matmul(0, k, 1)
+            if k > 0:
+                b_sq(k - 1, 1)
+            z_matmul(1, k, 1)
+            if k > 1:
+                b_out(k - 2, NT, NT)
+            if k > 0:
+                z_matmul(2, k, 0)
+            h_gain(k + 1)
+            if k == 0:
+                wh_inter(2, 0)
+                widen(2, 1, range(NV2), True)
+            x_copy(k + 3)
+            b_u(k, 0)
+            b_exp(k, 1)
+            if k > 0:
+                b_f(k - 1, 0)
+                b_f(k - 1, 1)
+            h_matmul(k + 2)
+            b_tanh(k, 1)
+            if k > 0:
+                b_w_rest(k - 1)
+            h_quant(k + 1)
+            x_quant(k + 3)
+            z_matmul(0, k + 1, 0)
+            b_sq(k, 0)
+            z_matmul(1, k + 1, 0)
+            if k > 0:
+                b_wf(k - 1, slice(0, N))
+            h_tanh(k + 2)
+            if k == 0:
+                wh_quant(2, 0)
+                z_matmul(2, k, 0)
+                widen(2, 1, range(NV2, 4))
+                wh_inter(2, 1)
+            b_u(k, 1)
+        k = NB - 1
+        b_clamp(k)
+        b_w(k)
+        b_out(k - 1, 0, NT)
+        z_matmul(2, k, 1)
+        b_sq(k, 1)
+        b_out(k - 1, NT, NT)
+        b_f(k, 0)
+        b_f(k, 1)
+        b_w_rest(k)
+        b_wf(k, slice(0, NT))
+        b_wf(k, slice(NT, N))
+        b_out(k, 0, NT)
+        b_out(k, NT, NT // 2)
+        b_out(k, NT + NT // 2, NT // 2)

@@ -22,9 +22,9 @@ NH = N // NT
 Z2B = 3
 UB = 1
 AUXB = 1
-NV = 1
-NV2 = 2
-GCUT = 128
+NV = 0
+GC0 = 256
+GCUT = 0
 
 
 def tile_escmdoublyrobusterrormap_kernel(tc, x, w, g, wh_bytes, wh_scale, o, y, out):
@@ -64,9 +64,9 @@ def tile_escmdoublyrobusterrormap_kernel(tc, x, w, g, wh_bytes, wh_scale, o, y, 
             nc.sync.dma_start(out=d[i][:], in_=src[P * i:P * (i + 1), :])
 
         load_wh(0, 2)
+        load_wh(1)
         load_w(0)
         load_rows(x_sb, x, "x", 0)
-        load_wh(1)
         load_w(1)
         load_rows(x_sb, x, "x", 1)
         load_wh(2)
@@ -84,9 +84,9 @@ def tile_escmdoublyrobusterrormap_kernel(tc, x, w, g, wh_bytes, wh_scale, o, y, 
         nc.gpsimd.tensor_scalar(out=neg2[:], in0=ident[:], scalar1=-2.0, scalar2=0.0, op0=ALU.mult, op1=ALU.add)
         ident_bf = const.tile([P, P], BF16, name="ident_bf")
         nc.gpsimd.tensor_scalar(out=ident_bf[:], in0=ident[:], scalar1=1.0, scalar2=0.0, op0=ALU.mult, op1=ALU.add)
-        g_ps = psum.tile([P, 4], F32, name="g_ps")
+        g_ps = psum.tile([P, P, 4], F32, name="g_ps")
 
-        w_g = {}
+        w_g = const.tile([P, 2, 4 * H], BF16, align_bytes=64, name="w_g")
         w_q = const.tile([P, 2, H], U32, align_bytes=64, name="w_q")
         w_s = const.tile([P, 2, H], U8, align_bytes=64, name="w_s")
         x_g = {}
@@ -104,14 +104,17 @@ def tile_escmdoublyrobusterrormap_kernel(tc, x, w, g, wh_bytes, wh_scale, o, y, 
         hg = {}
 
         def w_inter(c):
-            w_g[c] = work.tile([P, 4 * H], BF16, name="w_g", align_bytes=64, bufs=2)
             nc.vector.tensor_copy(
-                out=w_g[c][:].rearrange("p (t m j) -> p t m j", t=4, j=4),
+                out=w_g[:, c, :].rearrange("p (t m j) -> p t m j", t=4, j=4),
                 in_=w_raw[c][:].rearrange("p j (m t) -> p t m j", t=4),
             )
 
-        def w_quant(c):
-            nc.vector.quantize_mx(out=w_q[:, c, :].bitcast(FP8X4), scales=w_s[:, c, :], in_=w_g[c][:])
+        def w_quant():
+            nc.vector.quantize_mx(
+                out=w_q[:].rearrange("p c n -> p (c n)").bitcast(FP8X4),
+                scales=w_s[:].rearrange("p c n -> p (c n)"),
+                in_=w_g[:].rearrange("p c n -> p (c n)"),
+            )
 
         def x_trans(i):
             if i >= NB:
@@ -131,7 +134,7 @@ def tile_escmdoublyrobusterrormap_kernel(tc, x, w, g, wh_bytes, wh_scale, o, y, 
                 in_=xt[i][:].rearrange("p c u r -> p c r u"),
             )
 
-        def x_quant(i):
+        def x_quant(i, count):
             if i >= NB:
                 return
             nc.vector.quantize_mx(
@@ -166,7 +169,7 @@ def tile_escmdoublyrobusterrormap_kernel(tc, x, w, g, wh_bytes, wh_scale, o, y, 
             if i >= NB:
                 return
             hg[i] = work.tile([P, P, 4], BF16, name="hg", align_bytes=64)
-            nc.vector.tensor_tensor(out=hg[i][:], in0=th[i][:], in1=g_ps[:].unsqueeze(1).to_broadcast([P, P, 4]), op=ALU.mult)
+            nc.vector.tensor_tensor(out=hg[i][:], in0=th[i][:], in1=g_ps[:], op=ALU.mult)
 
         def h_quant(i):
             if i >= NB:
@@ -175,24 +178,25 @@ def tile_escmdoublyrobusterrormap_kernel(tc, x, w, g, wh_bytes, wh_scale, o, y, 
                 out=h_q[:, i, :].bitcast(FP8X4), scales=h_s[:, i, :], in_=hg[i][:].rearrange("p n t -> p (n t)")
             )
 
-        def wh_widen(t, h, j, on_vector):
-            if (t, h) not in wh_p:
-                wh_p[t, h] = work.tile([P, 4, NT], BF16, name="wh_p", bufs=4)
-            src = wh_b[t][:, j, NT * h:NT * (h + 1)].bitcast(FP8)
+        def wh_widen(t, j, on_vector, cols=slice(0, N)):
+            if t not in wh_p:
+                wh_p[t] = const.tile([P, 4, N], BF16, name="wh_p%d" % t)
+            src = wh_b[t][:, j, cols].bitcast(FP8)
             if on_vector:
-                nc.vector.tensor_scalar(out=wh_p[t, h][:, j, :], in0=src, scalar1=s_sb[:, j:j + 1], scalar2=None, op0=ALU.mult)
+                nc.vector.tensor_scalar(out=wh_p[t][:, j, cols], in0=src, scalar1=s_sb[:, j:j + 1], scalar2=None, op0=ALU.mult)
             else:
-                nc.scalar.activation(out=wh_p[t, h][:, j, :], in_=src, func=ACT.Copy, scale=s_sb[:, j:j + 1])
+                nc.scalar.activation(out=wh_p[t][:, j, cols], in_=src, func=ACT.Copy, scale=s_sb[:, j:j + 1])
 
-        def wh_inter(t, h):
-            wh_g[t, h] = work.tile([P, NT, 4], BF16, name="wh_g", align_bytes=64, bufs=3)
-            nc.vector.tensor_copy(out=wh_g[t, h][:].rearrange("p (c i) j -> p c j i", i=4), in_=wh_p[t, h][:].rearrange("p j (c i) -> p c j i", i=4))
+        def wh_inter(t, cols):
+            if t not in wh_g:
+                wh_g[t] = work.tile([P, N, 4], BF16, name="wh_g", align_bytes=64, bufs=2)
+            nc.vector.tensor_copy(out=wh_g[t][:, cols, :].rearrange("p (c i) j -> p c j i", i=4), in_=wh_p[t][:, :, cols].rearrange("p j (c i) -> p c j i", i=4))
 
-        def wh_quant(t, h):
+        def wh_quant(t, cols):
             nc.vector.quantize_mx(
-                out=wh_q[:, t, NT * h:NT * (h + 1)].bitcast(FP8X4),
-                scales=wh_s[:, t, NT * h:NT * (h + 1)],
-                in_=wh_g[t, h][:].rearrange("p n j -> p (n j)"),
+                out=wh_q[:, t, cols].bitcast(FP8X4),
+                scales=wh_s[:, t, cols],
+                in_=wh_g[t][:, cols, :].rearrange("p n j -> p (n j)"),
             )
 
         z = {}
@@ -258,10 +262,10 @@ def tile_escmdoublyrobusterrormap_kernel(tc, x, w, g, wh_bytes, wh_scale, o, y, 
             nc.vector.tensor_scalar(out=ee[i][:], in0=ee[i][:], scalar1=4.0, scalar2=1.0, op0=ALU.min, op1=ALU.add)
 
         def pool_share(i):
-            return N - GCUT * ((i == 0) * 2 + (i + 2 >= NB))
+            return N - GC0 * (i == 0) - GCUT * (i + 2 >= NB)
 
         def b_w(i):
-            ww[i] = work.tile([P, N], F32, name="ww", bufs=2)
+            ww[i] = work.tile([P, N], F32, name="ww", bufs=3)
             c = slice(0, pool_share(i))
             nc.gpsimd.tensor_tensor(out=ww[i][:, c], in0=ee[i][:, c], in1=o_sb[i][:, c], op=ALU.mult)
 
@@ -280,73 +284,66 @@ def tile_escmdoublyrobusterrormap_kernel(tc, x, w, g, wh_bytes, wh_scale, o, y, 
 
         def b_out(i, c0, width):
             h = c0 // NT
-            ot = work.tile([P, width], F32, name="ot", bufs=4)
-            nc.vector.tensor_tensor(out=ot[:], in0=z[2, i, h][:, c0 - NT * h:c0 - NT * h + width], in1=ff[i][:, c0:c0 + width], op=ALU.add)
-            nc.sync.dma_start(out=out[P * i:P * (i + 1), c0:c0 + width], in_=ot[:])
+            nc.vector.tensor_tensor(out=ww[i][:, c0:c0 + width], in0=z[2, i, h][:, c0 - NT * h:c0 - NT * h + width], in1=ff[i][:, c0:c0 + width], op=ALU.add)
+            nc.sync.dma_start(out=out[P * i:P * (i + 1), c0:c0 + width], in_=ww[i][:, c0:c0 + width])
 
 
-        def widen(t, h, planes=range(4), on_vector=False):
-            for j in planes:
-                wh_widen(t, h, j, on_vector)
-
-        wh_widen(0, 0, 0, True)
-        wh_widen(0, 0, 1, False)
-        wh_widen(0, 1, 0, True)
-        wh_widen(0, 1, 1, False)
-        wh_widen(0, 0, 2, True)
-        wh_widen(0, 0, 3, False)
-        wh_widen(0, 1, 2, True)
-        wh_widen(0, 1, 3, False)
+        lo, hi, both = slice(0, NT), slice(NT, N), slice(0, N)
+        for j in (0, 2):
+            wh_widen(0, j, True)
+        for cols in (lo, hi):
+            for j in (1, 3):
+                wh_widen(0, j, False, cols)
         x_trans(0)
-        nc.tensor.matmul(out=g_ps[:], lhsT=ident_bf[:], rhs=g_bf[:], start=True, stop=True)
+        nc.tensor.matmul(out=g_ps[:], lhsT=ident_bf[:], rhs=g_bf[:].unsqueeze(1).to_broadcast([P, P, 4]), start=True, stop=True)
         x_trans(1)
+        wh_inter(0, lo)
+        wh_inter(0, hi)
         w_inter(0)
-        x_copy(0)
-        wh_inter(0, 0)
-        w_quant(0)
-        widen(1, 0)
+        for j in range(3):
+            wh_widen(1, j, False)
         w_inter(1)
+        x_copy(0)
         x_trans(2)
-        x_quant(0)
-        w_quant(1)
+        x_quant(0, 1)
+        w_quant()
         h_matmul(0)
+        wh_widen(1, 3, False)
         x_copy(1)
-        widen(1, 1)
-        wh_inter(0, 1)
-        x_quant(1)
+        wh_quant(0, both)
+        x_quant(1, 1)
         h_matmul(1)
-        wh_quant(0, 0)
+        wh_widen(2, 0, False)
+        wh_widen(2, 1, False)
         h_tanh(0)
+        wh_inter(1, lo)
         x_copy(2)
-        wh_inter(1, 0)
+        wh_inter(1, hi)
         h_gain(0)
-        widen(2, 0, range(4 - NV), False)
-        wh_quant(1, 0)
+        wh_quant(1, lo)
         h_quant(0)
-        x_quant(2)
-        wh_inter(1, 1)
-        wh_quant(0, 1)
-        h_tanh(1)
         z_matmul(0, 0, 0)
         z_matmul(1, 0, 0)
-        wh_quant(1, 1)
-        widen(2, 0, range(4 - NV, 4), True)
+        h_tanh(1)
+        wh_widen(2, 2, NV > 1)
+        x_quant(2, 1)
+        wh_quant(1, hi)
+        wh_widen(2, 3, NV > 0)
 
         for k in range(NB):
             b_exp(k, 0)
             x_trans(k + 3)
-            if k == 1:
-                wh_quant(2, 1)
-                z_matmul(2, 0, 1)
             if k > 0:
                 b_clamp(k - 1)
                 b_w(k - 1)
             if k > 1:
                 b_out(k - 2, 0, NT)
             b_tanh(k, 0)
-            if k > 1:
-                z_matmul(2, k - 1, 1)
             z_matmul(0, k, 1)
+            if k == 1:
+                z_matmul(2, 0, 0)
+            if k > 0:
+                z_matmul(2, k - 1, 1)
             if k > 0:
                 b_sq(k - 1, 1)
             z_matmul(1, k, 1)
@@ -356,8 +353,7 @@ def tile_escmdoublyrobusterrormap_kernel(tc, x, w, g, wh_bytes, wh_scale, o, y, 
                 z_matmul(2, k, 0)
             h_gain(k + 1)
             if k == 0:
-                wh_inter(2, 0)
-                widen(2, 1, range(NV2), True)
+                wh_inter(2, lo)
             x_copy(k + 3)
             b_u(k, 0)
             b_exp(k, 1)
@@ -369,7 +365,9 @@ def tile_escmdoublyrobusterrormap_kernel(tc, x, w, g, wh_bytes, wh_scale, o, y, 
             if k > 0:
                 b_w_rest(k - 1)
             h_quant(k + 1)
-            x_quant(k + 3)
+            if k == 0:
+                wh_inter(2, hi)
+            x_quant(k + 3, 1)
             z_matmul(0, k + 1, 0)
             b_sq(k, 0)
             z_matmul(1, k + 1, 0)
@@ -377,10 +375,7 @@ def tile_escmdoublyrobusterrormap_kernel(tc, x, w, g, wh_bytes, wh_scale, o, y, 
                 b_wf(k - 1, slice(0, N))
             h_tanh(k + 2)
             if k == 0:
-                wh_quant(2, 0)
-                z_matmul(2, k, 0)
-                widen(2, 1, range(NV2, 4))
-                wh_inter(2, 1)
+                wh_quant(2, both)
             b_u(k, 1)
         k = NB - 1
         b_clamp(k)

@@ -22,8 +22,9 @@ NH = N // NT
 Z2B = 3
 UB = 1
 AUXB = 1
-NV = 0
+NV = 1
 GC0 = 256
+LASTW = 256
 GCUT = 0
 
 
@@ -64,12 +65,12 @@ def tile_escmdoublyrobusterrormap_kernel(tc, x, w, g, wh_bytes, wh_scale, o, y, 
             nc.sync.dma_start(out=d[i][:], in_=src[P * i:P * (i + 1), :])
 
         load_wh(0, 2)
-        load_wh(1)
+        load_wh(1, 2)
         load_w(0)
-        load_rows(x_sb, x, "x", 0)
         load_w(1)
-        load_rows(x_sb, x, "x", 1)
+        load_rows(x_sb, x, "x", 0)
         load_wh(2)
+        load_rows(x_sb, x, "x", 1)
         load_rows(x_sb, x, "x", 2)
         load_rows(x_sb, x, "x", 3)
         for i in range(NB):
@@ -94,6 +95,7 @@ def tile_escmdoublyrobusterrormap_kernel(tc, x, w, g, wh_bytes, wh_scale, o, y, 
         x_s = const.tile([P, NB, 2, P], U8, align_bytes=64, name="x_s")
         wh_p = {}
         wh_g = {}
+        wh_ps = {}
         wh_q = const.tile([P, T, N], U32, align_bytes=64, name="wh_q")
         wh_s = const.tile([P, T, N], U8, align_bytes=64, name="wh_s")
         h_q = const.tile([P, NB, P], U32, align_bytes=64, name="h_q")
@@ -104,10 +106,10 @@ def tile_escmdoublyrobusterrormap_kernel(tc, x, w, g, wh_bytes, wh_scale, o, y, 
         hg = {}
 
         def w_inter(c):
-            nc.vector.tensor_copy(
-                out=w_g[:, c, :].rearrange("p (t m j) -> p t m j", t=4, j=4),
-                in_=w_raw[c][:].rearrange("p j (m t) -> p t m j", t=4),
-            )
+            src = w_raw[c][:].rearrange("p j (a m u t) -> p u a j m t", m=2, u=2, t=2)
+            dst = w_g[:, c, :].rearrange("p (u t a m j) -> p u a j m t", u=2, t=2, m=2, j=4)
+            for u in range(2):
+                nc.vector.tensor_copy(out=dst[:, u], in_=src[:, u])
 
         def w_quant():
             nc.vector.quantize_mx(
@@ -191,6 +193,26 @@ def tile_escmdoublyrobusterrormap_kernel(tc, x, w, g, wh_bytes, wh_scale, o, y, 
             if t not in wh_g:
                 wh_g[t] = work.tile([P, N, 4], BF16, name="wh_g", align_bytes=64, bufs=2)
             nc.vector.tensor_copy(out=wh_g[t][:, cols, :].rearrange("p (c i) j -> p c j i", i=4), in_=wh_p[t][:, :, cols].rearrange("p j (c i) -> p c j i", i=4))
+
+        def wh_turn(t, a):
+            wh_ps[a] = psum.tile([P, 2, P, 4], BF16, name="wh_ps", tag=("z0", "z1", "up", "z0")[a], bufs=1)
+            for b in range(2):
+                c0 = 2 * P * a + P * b
+                nc.tensor.matmul(
+                    out=wh_ps[a][:, b, :, :].rearrange("p n j -> p (n j)"),
+                    lhsT=ident_bf[:],
+                    rhs=wh_p[t][:, :, c0:c0 + P].rearrange("p j n -> p n j"),
+                    start=True,
+                    stop=True,
+                )
+
+        def wh_copy(t, a):
+            if t not in wh_g:
+                wh_g[t] = work.tile([P, N, 4], BF16, name="wh_g", align_bytes=64, bufs=2)
+            nc.scalar.copy(
+                out=wh_g[t][:, 2 * P * a:2 * P * (a + 1), :].rearrange("p n j -> p (n j)"),
+                in_=wh_ps[a][:].rearrange("p b n j -> p (b n j)"),
+            )
 
         def wh_quant(t, cols):
             nc.vector.quantize_mx(
@@ -289,46 +311,52 @@ def tile_escmdoublyrobusterrormap_kernel(tc, x, w, g, wh_bytes, wh_scale, o, y, 
 
 
         lo, hi, both = slice(0, NT), slice(NT, N), slice(0, N)
+        nc.tensor.matmul(out=g_ps[:], lhsT=ident_bf[:], rhs=g_bf[:].unsqueeze(1).to_broadcast([P, P, 4]), start=True, stop=True)
         for j in (0, 2):
             wh_widen(0, j, True)
         for cols in (lo, hi):
             for j in (1, 3):
                 wh_widen(0, j, False, cols)
+        wh_turn(0, 0)
+        wh_turn(0, 1)
         x_trans(0)
-        nc.tensor.matmul(out=g_ps[:], lhsT=ident_bf[:], rhs=g_bf[:].unsqueeze(1).to_broadcast([P, P, 4]), start=True, stop=True)
-        x_trans(1)
-        wh_inter(0, lo)
-        wh_inter(0, hi)
-        w_inter(0)
+        wh_turn(0, 2)
         for j in range(3):
-            wh_widen(1, j, False)
+            wh_widen(1, j, j < 2)
+        w_inter(0)
         w_inter(1)
+        wh_widen(1, 3, False)
+        wh_copy(0, 0)
+        wh_turn(0, 3)
+        x_trans(1)
         x_copy(0)
-        x_trans(2)
+        wh_copy(0, 1)
+        wh_inter(1, lo)
         x_quant(0, 1)
         w_quant()
+        wh_widen(2, 0, False)
+        wh_copy(0, 2)
+        wh_copy(0, 3)
         h_matmul(0)
-        wh_widen(1, 3, False)
+        x_trans(2)
         x_copy(1)
+        wh_inter(1, hi)
         wh_quant(0, both)
         x_quant(1, 1)
         h_matmul(1)
-        wh_widen(2, 0, False)
-        wh_widen(2, 1, False)
         h_tanh(0)
-        wh_inter(1, lo)
         x_copy(2)
-        wh_inter(1, hi)
+        wh_widen(2, 1, False)
         h_gain(0)
         wh_quant(1, lo)
         h_quant(0)
+        wh_widen(2, 2, False)
         z_matmul(0, 0, 0)
         z_matmul(1, 0, 0)
         h_tanh(1)
-        wh_widen(2, 2, NV > 1)
+        wh_widen(2, 3, NV > 0)
         x_quant(2, 1)
         wh_quant(1, hi)
-        wh_widen(2, 3, NV > 0)
 
         for k in range(NB):
             b_exp(k, 0)
@@ -390,5 +418,5 @@ def tile_escmdoublyrobusterrormap_kernel(tc, x, w, g, wh_bytes, wh_scale, o, y, 
         b_wf(k, slice(0, NT))
         b_wf(k, slice(NT, N))
         b_out(k, 0, NT)
-        b_out(k, NT, NT // 2)
-        b_out(k, NT + NT // 2, NT // 2)
+        b_out(k, NT, NT - LASTW)
+        b_out(k, N - LASTW, LASTW)

@@ -25,6 +25,7 @@ AUXB = 1
 NV = 1
 GC0 = 256
 LASTW = 256
+GX = 0
 GCUT = 0
 
 
@@ -232,7 +233,10 @@ def tile_escmdoublyrobusterrormap_kernel(tc, x, w, g, wh_bytes, wh_scale, o, y, 
         def z_matmul(t, i, h):
             if i >= NB:
                 return
-            z[t, i, h] = psum.tile([P, NT], F32, name="z%d" % t, bufs=Z2B if t == 2 else 1)
+            if (t, h) == (2, 1) and i >= NB - 2:
+                z[t, i, h] = psum.tile([P, NT], F32, name="z_late", tag="aux" if i == NB - 2 else "g_ps", bufs=1)
+            else:
+                z[t, i, h] = psum.tile([P, NT], F32, name="z%d" % t, bufs=Z2B if t == 2 else 1)
             if t == 1:
                 for c in range(4):
                     cols = slice(NT * h + P * c, NT * h + P * (c + 1))
@@ -286,6 +290,14 @@ def tile_escmdoublyrobusterrormap_kernel(tc, x, w, g, wh_bytes, wh_scale, o, y, 
         def pool_share(i):
             return N - GC0 * (i == 0) - GCUT * (i + 2 >= NB)
 
+        def pool_extra(i):
+            return GX if 0 < i < NB - 2 else 0
+
+        def g_wf(i):
+            if pool_extra(i):
+                c = slice(0, pool_extra(i))
+                nc.gpsimd.tensor_tensor(out=ff[i][:, c], in0=ww[i][:, c], in1=ff[i][:, c], op=ALU.mult)
+
         def b_w(i):
             ww[i] = work.tile([P, N], F32, name="ww", bufs=3)
             c = slice(0, pool_share(i))
@@ -321,16 +333,18 @@ def tile_escmdoublyrobusterrormap_kernel(tc, x, w, g, wh_bytes, wh_scale, o, y, 
         wh_turn(0, 1)
         x_trans(0)
         wh_turn(0, 2)
-        for j in range(3):
-            wh_widen(1, j, j < 2)
+        for j in range(2):
+            wh_widen(1, j, True)
+        wh_widen(1, 2, True, lo)
+        wh_widen(1, 2, False, hi)
         w_inter(0)
         w_inter(1)
         wh_widen(1, 3, False)
         wh_copy(0, 0)
         wh_turn(0, 3)
         x_trans(1)
-        x_copy(0)
         wh_copy(0, 1)
+        x_copy(0)
         wh_inter(1, lo)
         x_quant(0, 1)
         w_quant()
@@ -344,49 +358,43 @@ def tile_escmdoublyrobusterrormap_kernel(tc, x, w, g, wh_bytes, wh_scale, o, y, 
         wh_quant(0, both)
         x_quant(1, 1)
         h_matmul(1)
+        wh_widen(2, 1, False)
         h_tanh(0)
         x_copy(2)
-        wh_widen(2, 1, False)
-        h_gain(0)
         wh_quant(1, lo)
+        h_gain(0)
+        wh_widen(2, 3, True)
         h_quant(0)
         wh_widen(2, 2, False)
         z_matmul(0, 0, 0)
         z_matmul(1, 0, 0)
         h_tanh(1)
-        wh_widen(2, 3, NV > 0)
         x_quant(2, 1)
         wh_quant(1, hi)
 
         for k in range(NB):
             b_exp(k, 0)
             x_trans(k + 3)
-            if k > 0:
-                b_clamp(k - 1)
-                b_w(k - 1)
             if k > 1:
                 b_out(k - 2, 0, NT)
             b_tanh(k, 0)
             z_matmul(0, k, 1)
-            if k == 1:
-                z_matmul(2, 0, 0)
             if k > 0:
                 z_matmul(2, k - 1, 1)
-            if k > 0:
                 b_sq(k - 1, 1)
             z_matmul(1, k, 1)
             if k > 1:
                 b_out(k - 2, NT, NT)
             if k > 0:
                 z_matmul(2, k, 0)
-            h_gain(k + 1)
+            if k != 1:
+                h_gain(k + 1)
             if k == 0:
                 wh_inter(2, lo)
             x_copy(k + 3)
             b_u(k, 0)
             b_exp(k, 1)
             if k > 0:
-                b_f(k - 1, 0)
                 b_f(k - 1, 1)
             h_matmul(k + 2)
             b_tanh(k, 1)
@@ -396,23 +404,28 @@ def tile_escmdoublyrobusterrormap_kernel(tc, x, w, g, wh_bytes, wh_scale, o, y, 
             if k == 0:
                 wh_inter(2, hi)
             x_quant(k + 3, 1)
+            if k == 0:
+                wh_quant(2, lo)
             z_matmul(0, k + 1, 0)
             b_sq(k, 0)
             z_matmul(1, k + 1, 0)
+            b_clamp(k)
+            b_w(k)
             if k > 0:
-                b_wf(k - 1, slice(0, N))
+                b_wf(k - 1, slice(pool_extra(k - 1), N))
             h_tanh(k + 2)
-            if k == 0:
-                wh_quant(2, both)
             b_u(k, 1)
+            if k == 0:
+                wh_quant(2, hi)
+                z_matmul(2, 0, 0)
+                h_gain(2)
+            b_f(k, 0)
+            g_wf(k)
         k = NB - 1
-        b_clamp(k)
-        b_w(k)
-        b_out(k - 1, 0, NT)
         z_matmul(2, k, 1)
+        b_out(k - 1, 0, NT)
         b_sq(k, 1)
         b_out(k - 1, NT, NT)
-        b_f(k, 0)
         b_f(k, 1)
         b_w_rest(k)
         b_wf(k, slice(0, NT))

@@ -25,7 +25,7 @@ AUXB = 1
 NV = 1
 GC0 = 256
 LASTW = 256
-GX = 0
+GX = 128
 GCUT = 0
 
 
@@ -41,9 +41,6 @@ def tile_escmdoublyrobusterrormap_kernel(tc, x, w, g, wh_bytes, wh_scale, o, y, 
         nc.scalar.dma_start(out=s_sb[:], in_=wh_scale.rearrange("o (p t) q -> p (o t q)", t=4))
         g_bf = const.tile([P, 4], BF16, name="g_bf")
         nc.scalar.dma_start(out=g_bf[:], in_=g.rearrange("(p t) -> p t", t=4))
-        warm = const.tile([P, 1], F32, name="warm")
-        nc.vector.memset(warm[:], 0.0)
-        nc.scalar.activation(out=warm[:], in_=warm[:], func=ACT.Exp)
 
         w_raw = {}
         wh_b = {}
@@ -83,7 +80,7 @@ def tile_escmdoublyrobusterrormap_kernel(tc, x, w, g, wh_bytes, wh_scale, o, y, 
         ident = const.tile([P, P], F32, name="ident")
         make_identity(nc, ident[:])
         neg2 = const.tile([P, P], BF16, name="neg2")
-        nc.gpsimd.tensor_scalar(out=neg2[:], in0=ident[:], scalar1=-2.0, scalar2=0.0, op0=ALU.mult, op1=ALU.add)
+        nc.scalar.activation(out=neg2[:], in_=ident[:], func=ACT.Copy, scale=-2.0)
         ident_bf = const.tile([P, P], BF16, name="ident_bf")
         nc.gpsimd.tensor_scalar(out=ident_bf[:], in0=ident[:], scalar1=1.0, scalar2=0.0, op0=ALU.mult, op1=ALU.add)
         g_ps = psum.tile([P, P, 4], F32, name="g_ps")

@@ -16,17 +16,15 @@ ACT = mybir.ActivationFunctionType
 ALU = mybir.AluOpType
 
 P = 128
-NT = 512
-NB = B // P
-NH = N // NT
-Z2B = 3
-UB = 1
-AUXB = 1
-NV = 1
-GC0 = 256
-LASTW = 256
-GX = 128
-GCUT = 0
+BANK = 512
+TILES = B // P
+PASSES = D // 512
+LO, HI, BOTH = slice(0, BANK), slice(BANK, N), slice(0, N)
+HEAD_P, HEAD_ERR, HEAD_E = 0, 1, 2
+
+E_BANKS = 3
+FIRST_REST, LAST_REST = 256, 128
+LAST_STORE = 256
 
 
 def tile_escmdoublyrobusterrormap_kernel(tc, x, w, g, wh_bytes, wh_scale, o, y, out):
@@ -37,44 +35,39 @@ def tile_escmdoublyrobusterrormap_kernel(tc, x, w, g, wh_bytes, wh_scale, o, y, 
         psum = ctx.enter_context(tc.psum_pool(name="psum", bufs=1))
         ctx.enter_context(tc.manual_schedule())
 
-        s_sb = const.tile([P, 4], F32, name="s_sb")
-        nc.scalar.dma_start(out=s_sb[:], in_=wh_scale.rearrange("o (p t) q -> p (o t q)", t=4))
-        g_bf = const.tile([P, 4], BF16, name="g_bf")
-        nc.scalar.dma_start(out=g_bf[:], in_=g.rearrange("(p t) -> p t", t=4))
+        scale = const.tile([P, 4], F32, name="s_sb")
+        nc.scalar.dma_start(out=scale[:], in_=wh_scale.rearrange("o (p j) q -> p (o j q)", j=4))
+        gain = const.tile([P, 4], BF16, name="g_bf")
+        nc.scalar.dma_start(out=gain[:], in_=g.rearrange("(p j) -> p j", j=4))
 
-        w_raw = {}
-        wh_b = {}
-        x_sb = {}
-        o_sb = {}
-        y_sb = {}
+        w_raw, wh_raw, x_sb, o_sb, y_sb = {}, {}, {}, {}, {}
 
         def load_w(c):
             w_raw[c] = const.tile([P, 4, H], BF16, name="w_raw%d" % c)
             nc.sync.dma_start(out=w_raw[c][:], in_=w[512 * c:512 * (c + 1), :].rearrange("(p j) c -> p j c", j=4))
 
-        def load_wh(t, parts=1):
-            wh_b[t] = const.tile([P, 4, N], U8, name="wh_b%d" % t)
-            src = wh_bytes[t].rearrange("(p j) n -> p j n", j=4)
-            for j0 in range(0, 4, 4 // parts):
-                nc.sync.dma_start(out=wh_b[t][:, j0:j0 + 4 // parts, :], in_=src[:, j0:j0 + 4 // parts, :])
+        def load_wh(t, planes_per_dma):
+            wh_raw[t] = const.tile([P, 4, N], U8, name="wh_b%d" % t)
+            rows = wh_bytes[t].rearrange("(p j) n -> p j n", j=4)
+            for j in range(0, 4, planes_per_dma):
+                nc.sync.dma_start(out=wh_raw[t][:, j:j + planes_per_dma, :], in_=rows[:, j:j + planes_per_dma, :])
 
-        def load_rows(d, src, label, i):
-            d[i] = const.tile([P, N], BF16, name="%s_%d" % (label, i))
-            nc.sync.dma_start(out=d[i][:], in_=src[P * i:P * (i + 1), :])
+        def load_rows(tiles, src, label, i):
+            tiles[i] = const.tile([P, N], BF16, name="%s_%d" % (label, i))
+            nc.sync.dma_start(out=tiles[i][:], in_=src[P * i:P * (i + 1), :])
 
-        load_wh(0, 2)
-        load_wh(1, 2)
+        load_wh(HEAD_P, 2)
+        load_wh(HEAD_ERR, 2)
         load_w(0)
         load_w(1)
         load_rows(x_sb, x, "x", 0)
-        load_wh(2)
-        load_rows(x_sb, x, "x", 1)
-        load_rows(x_sb, x, "x", 2)
-        load_rows(x_sb, x, "x", 3)
-        for i in range(NB):
+        load_wh(HEAD_E, 4)
+        for i in range(1, 4):
+            load_rows(x_sb, x, "x", i)
+        for i in range(TILES):
             load_rows(y_sb, y, "y", i)
             load_rows(o_sb, o, "o", i)
-            if i + 4 < NB:
+            if i + 4 < TILES:
                 load_rows(x_sb, x, "x", i + 4)
 
         ident = const.tile([P, P], F32, name="ident")
@@ -83,59 +76,56 @@ def tile_escmdoublyrobusterrormap_kernel(tc, x, w, g, wh_bytes, wh_scale, o, y, 
         nc.scalar.activation(out=neg2[:], in_=ident[:], func=ACT.Copy, scale=-2.0)
         ident_bf = const.tile([P, P], BF16, name="ident_bf")
         nc.gpsimd.tensor_scalar(out=ident_bf[:], in0=ident[:], scalar1=1.0, scalar2=0.0, op0=ALU.mult, op1=ALU.add)
-        g_ps = psum.tile([P, P, 4], F32, name="g_ps")
+        gain_ps = psum.tile([P, P, 4], F32, name="g_ps")
 
-        w_g = const.tile([P, 2, 4 * H], BF16, align_bytes=64, name="w_g")
-        w_q = const.tile([P, 2, H], U32, align_bytes=64, name="w_q")
-        w_s = const.tile([P, 2, H], U8, align_bytes=64, name="w_s")
-        x_g = {}
-        x_q = const.tile([P, NB, 2, P], U32, align_bytes=64, name="x_q")
-        x_s = const.tile([P, NB, 2, P], U8, align_bytes=64, name="x_s")
-        wh_p = {}
-        wh_g = {}
-        wh_ps = {}
+        w_g = const.tile([P, PASSES, 4 * H], BF16, align_bytes=64, name="w_g")
+        w_q = const.tile([P, PASSES, H], U32, align_bytes=64, name="w_q")
+        w_s = const.tile([P, PASSES, H], U8, align_bytes=64, name="w_s")
+        x_q = const.tile([P, TILES, PASSES, P], U32, align_bytes=64, name="x_q")
+        x_s = const.tile([P, TILES, PASSES, P], U8, align_bytes=64, name="x_s")
         wh_q = const.tile([P, T, N], U32, align_bytes=64, name="wh_q")
         wh_s = const.tile([P, T, N], U8, align_bytes=64, name="wh_s")
-        h_q = const.tile([P, NB, P], U32, align_bytes=64, name="h_q")
-        h_s = const.tile([P, NB, P], U8, align_bytes=64, name="h_s")
-        xt = {}
-        ht = {}
-        th = {}
-        hg = {}
+        h_q = const.tile([P, TILES, P], U32, align_bytes=64, name="h_q")
+        h_s = const.tile([P, TILES, P], U8, align_bytes=64, name="h_s")
+        x_t, x_g, h_pre, h_tanh, h_g = {}, {}, {}, {}, {}
+        wh_wide, wh_ps, wh_g = {}, {}, {}
 
-        def w_inter(c):
-            src = w_raw[c][:].rearrange("p j (a m u t) -> p u a j m t", m=2, u=2, t=2)
-            dst = w_g[:, c, :].rearrange("p (u t a m j) -> p u a j m t", u=2, t=2, m=2, j=4)
+        def w_interleave(c):
+            src = w_raw[c][:].rearrange("p j (a b u v) -> p u a j b v", b=2, u=2, v=2)
+            dst = w_g[:, c, :].rearrange("p (u v a b j) -> p u a j b v", u=2, v=2, b=2, j=4)
             for u in range(2):
                 nc.vector.tensor_copy(out=dst[:, u], in_=src[:, u])
 
-        def w_quant():
+        def w_quantize():
             nc.vector.quantize_mx(
                 out=w_q[:].rearrange("p c n -> p (c n)").bitcast(FP8X4),
                 scales=w_s[:].rearrange("p c n -> p (c n)"),
                 in_=w_g[:].rearrange("p c n -> p (c n)"),
             )
 
-        def x_trans(i):
-            if i >= NB:
+        def x_transpose(i):
+            if i >= TILES:
                 return
-            xt[i] = psum.tile([P, 2, 2, P], F32, name="xt", tag="z2" if i < 3 else "aux", bufs=Z2B if i < 3 else AUXB)
+            if i < E_BANKS:
+                x_t[i] = psum.tile([P, PASSES, 2, P], F32, name="xt", tag="z2", bufs=E_BANKS)
+            else:
+                x_t[i] = psum.tile([P, PASSES, 2, P], F32, name="xt", tag="aux")
             words = x_sb[i][:].bitcast(F32)
-            for c in range(2):
+            for c in range(PASSES):
                 for u in range(2):
-                    nc.tensor.transpose(xt[i][:, c, u, :], words[:, 256 * c + u:256 * (c + 1):2], ident[:])
+                    nc.tensor.transpose(x_t[i][:, c, u, :], words[:, 256 * c + u:256 * (c + 1):2], ident[:])
 
         def x_copy(i):
-            if i >= NB:
+            if i >= TILES:
                 return
-            x_g[i] = work.tile([P, 2 * P * 4], BF16, name="x_g", align_bytes=64)
+            x_g[i] = work.tile([P, PASSES * P * 4], BF16, name="x_g", align_bytes=64)
             nc.scalar.copy(
-                out=x_g[i][:].bitcast(F32).rearrange("p (c r u) -> p c r u", c=2, u=2),
-                in_=xt[i][:].rearrange("p c u r -> p c r u"),
+                out=x_g[i][:].bitcast(F32).rearrange("p (c r u) -> p c r u", c=PASSES, u=2),
+                in_=x_t[i][:].rearrange("p c u r -> p c r u"),
             )
 
-        def x_quant(i, count):
-            if i >= NB:
+        def x_quantize(i):
+            if i >= TILES:
                 return
             nc.vector.quantize_mx(
                 out=x_q[:, i, :, :].rearrange("p c r -> p (c r)").bitcast(FP8X4),
@@ -144,101 +134,112 @@ def tile_escmdoublyrobusterrormap_kernel(tc, x, w, g, wh_bytes, wh_scale, o, y, 
             )
 
         def h_matmul(i):
-            if i >= NB:
+            if i >= TILES:
                 return
-            ht[i] = psum.tile([P, 4, P], F32, name="ht", tag="up" if i == 1 else "aux", bufs=AUXB)
-            for t in range(4):
-                for c in range(2):
+            h_pre[i] = psum.tile([P, 4, P], F32, name="ht", tag="up" if i == 1 else "aux")
+            for s in range(4):
+                for c in range(PASSES):
                     nc.tensor.matmul_mx(
-                        out=ht[i][:, t, :],
-                        lhsT=w_q[:, c, P * t:P * (t + 1)].bitcast(FP8X4),
-                        lhsT_scale=w_s[:, c, P * t:P * (t + 1)],
+                        out=h_pre[i][:, s, :],
+                        lhsT=w_q[:, c, P * s:P * (s + 1)].bitcast(FP8X4),
+                        lhsT_scale=w_s[:, c, P * s:P * (s + 1)],
                         rhs=x_q[:, i, c, :].bitcast(FP8X4),
                         rhs_scale=x_s[:, i, c, :],
                         start=(c == 0),
-                        stop=(c == 1),
+                        stop=(c == PASSES - 1),
                     )
 
-        def h_tanh(i):
-            if i >= NB:
+        def h_activate(i):
+            if i >= TILES:
                 return
-            th[i] = work.tile([P, P, 4], F32, name="th")
-            nc.scalar.activation(out=th[i][:], in_=ht[i][:].rearrange("p t n -> p n t"), func=ACT.Tanh)
+            h_tanh[i] = work.tile([P, P, 4], F32, name="th")
+            nc.scalar.activation(out=h_tanh[i][:], in_=h_pre[i][:].rearrange("p s r -> p r s"), func=ACT.Tanh)
 
         def h_gain(i):
-            if i >= NB:
+            if i >= TILES:
                 return
-            hg[i] = work.tile([P, P, 4], BF16, name="hg", align_bytes=64)
-            nc.vector.tensor_tensor(out=hg[i][:], in0=th[i][:], in1=g_ps[:], op=ALU.mult)
+            h_g[i] = work.tile([P, P, 4], BF16, name="hg", align_bytes=64)
+            nc.vector.tensor_tensor(out=h_g[i][:], in0=h_tanh[i][:], in1=gain_ps[:], op=ALU.mult)
 
-        def h_quant(i):
-            if i >= NB:
+        def h_quantize(i):
+            if i >= TILES:
                 return
             nc.vector.quantize_mx(
-                out=h_q[:, i, :].bitcast(FP8X4), scales=h_s[:, i, :], in_=hg[i][:].rearrange("p n t -> p (n t)")
+                out=h_q[:, i, :].bitcast(FP8X4), scales=h_s[:, i, :], in_=h_g[i][:].rearrange("p r s -> p (r s)")
             )
 
-        def wh_widen(t, j, on_vector, cols=slice(0, N)):
-            if t not in wh_p:
-                wh_p[t] = const.tile([P, 4, N], BF16, name="wh_p%d" % t)
-            src = wh_b[t][:, j, cols].bitcast(FP8)
-            if on_vector:
-                nc.vector.tensor_scalar(out=wh_p[t][:, j, cols], in0=src, scalar1=s_sb[:, j:j + 1], scalar2=None, op0=ALU.mult)
-            else:
-                nc.scalar.activation(out=wh_p[t][:, j, cols], in_=src, func=ACT.Copy, scale=s_sb[:, j:j + 1])
+        def wide_tile(t):
+            if t not in wh_wide:
+                wh_wide[t] = const.tile([P, 4, N], BF16, name="wh_p%d" % t)
+            return wh_wide[t]
 
-        def wh_inter(t, cols):
+        def grouped_tile(t):
             if t not in wh_g:
                 wh_g[t] = work.tile([P, N, 4], BF16, name="wh_g", align_bytes=64, bufs=2)
-            nc.vector.tensor_copy(out=wh_g[t][:, cols, :].rearrange("p (c i) j -> p c j i", i=4), in_=wh_p[t][:, :, cols].rearrange("p j (c i) -> p c j i", i=4))
+            return wh_g[t]
 
-        def wh_turn(t, a):
-            wh_ps[a] = psum.tile([P, 2, P, 4], BF16, name="wh_ps", tag=("z0", "z1", "up", "z0")[a], bufs=1)
+        def widen_on_vector(t, j, cols):
+            nc.vector.tensor_scalar(
+                out=wide_tile(t)[:, j, cols],
+                in0=wh_raw[t][:, j, cols].bitcast(FP8),
+                scalar1=scale[:, j:j + 1],
+                scalar2=None,
+                op0=ALU.mult,
+            )
+
+        def widen_on_scalar(t, j, cols):
+            nc.scalar.activation(
+                out=wide_tile(t)[:, j, cols], in_=wh_raw[t][:, j, cols].bitcast(FP8), func=ACT.Copy, scale=scale[:, j:j + 1]
+            )
+
+        def wh_interleave(t, cols):
+            nc.vector.tensor_copy(
+                out=grouped_tile(t)[:, cols, :].rearrange("p (c i) j -> p c j i", i=4),
+                in_=wh_wide[t][:, :, cols].rearrange("p j (c i) -> p c j i", i=4),
+            )
+
+        def wh_turn(quarter):
+            wh_ps[quarter] = psum.tile([P, 2, P, 4], BF16, name="wh_ps", tag=("z0", "z1", "up")[quarter % 3])
             for b in range(2):
-                c0 = 2 * P * a + P * b
+                c0 = 2 * P * quarter + P * b
                 nc.tensor.matmul(
-                    out=wh_ps[a][:, b, :, :].rearrange("p n j -> p (n j)"),
+                    out=wh_ps[quarter][:, b, :, :].rearrange("p n j -> p (n j)"),
                     lhsT=ident_bf[:],
-                    rhs=wh_p[t][:, :, c0:c0 + P].rearrange("p j n -> p n j"),
+                    rhs=wh_wide[HEAD_P][:, :, c0:c0 + P].rearrange("p j n -> p n j"),
                     start=True,
                     stop=True,
                 )
 
-        def wh_copy(t, a):
-            if t not in wh_g:
-                wh_g[t] = work.tile([P, N, 4], BF16, name="wh_g", align_bytes=64, bufs=2)
+        def wh_copy(quarter):
             nc.scalar.copy(
-                out=wh_g[t][:, 2 * P * a:2 * P * (a + 1), :].rearrange("p n j -> p (n j)"),
-                in_=wh_ps[a][:].rearrange("p b n j -> p (b n j)"),
+                out=grouped_tile(HEAD_P)[:, 2 * P * quarter:2 * P * (quarter + 1), :].rearrange("p n j -> p (n j)"),
+                in_=wh_ps[quarter][:].rearrange("p b n j -> p (b n j)"),
             )
 
-        def wh_quant(t, cols):
+        def wh_quantize(t, cols):
             nc.vector.quantize_mx(
                 out=wh_q[:, t, cols].bitcast(FP8X4),
                 scales=wh_s[:, t, cols],
                 in_=wh_g[t][:, cols, :].rearrange("p n j -> p (n j)"),
             )
 
-        z = {}
-        tt = {}
-        ee = {}
-        uu = {}
-        er = {}
-        ww = {}
-        ff = {}
+        z, z1_tanh, inv_p, diff, err, weight, gap = {}, {}, {}, {}, {}, {}, {}
 
-        def z_matmul(t, i, h):
-            if i >= NB:
+        def half_cols(half):
+            return (LO, HI)[half]
+
+        def z_matmul(t, i, half):
+            if i >= TILES:
                 return
-            if (t, h) == (2, 1) and i >= NB - 2:
-                z[t, i, h] = psum.tile([P, NT], F32, name="z_late", tag="aux" if i == NB - 2 else "g_ps", bufs=1)
+            if t == HEAD_E and half == 1 and i >= TILES - 2:
+                z[t, i, half] = psum.tile([P, BANK], F32, name="z_late", tag="aux" if i == TILES - 2 else "g_ps")
             else:
-                z[t, i, h] = psum.tile([P, NT], F32, name="z%d" % t, bufs=Z2B if t == 2 else 1)
-            if t == 1:
+                z[t, i, half] = psum.tile([P, BANK], F32, name="z%d" % t, bufs=E_BANKS if t == HEAD_E else 1)
+            if t == HEAD_ERR:
                 for c in range(4):
-                    cols = slice(NT * h + P * c, NT * h + P * (c + 1))
+                    cols = slice(BANK * half + P * c, BANK * half + P * (c + 1))
                     nc.tensor.matmul_mx(
-                        out=z[t, i, h][:, P * c:P * (c + 1)],
+                        out=z[t, i, half][:, P * c:P * (c + 1)],
                         lhsT=wh_q[:, t, cols].bitcast(FP8X4),
                         lhsT_scale=wh_s[:, t, cols],
                         rhs=h_q[:, i, :].bitcast(FP8X4),
@@ -246,187 +247,183 @@ def tile_escmdoublyrobusterrormap_kernel(tc, x, w, g, wh_bytes, wh_scale, o, y, 
                         start=True,
                         stop=True,
                     )
-                return
-            nc.tensor.matmul_mx(
-                out=z[t, i, h][:],
-                lhsT=h_q[:, i, :].bitcast(FP8X4),
-                lhsT_scale=h_s[:, i, :],
-                rhs=wh_q[:, t, NT * h:NT * (h + 1)].bitcast(FP8X4),
-                rhs_scale=wh_s[:, t, NT * h:NT * (h + 1)],
-                start=True,
-                stop=True,
-            )
+            else:
+                nc.tensor.matmul_mx(
+                    out=z[t, i, half][:],
+                    lhsT=h_q[:, i, :].bitcast(FP8X4),
+                    lhsT_scale=h_s[:, i, :],
+                    rhs=wh_q[:, t, half_cols(half)].bitcast(FP8X4),
+                    rhs_scale=wh_s[:, t, half_cols(half)],
+                    start=True,
+                    stop=True,
+                )
 
-        def b_tanh(i, h):
-            if i >= NB:
-                return
-            tt[i, h] = work.tile([P, NT], F32, name="tt")
-            nc.scalar.activation(out=tt[i, h][:], in_=z[1, i, h][:], func=ACT.Tanh, scale=0.5)
+        def exp_z0(i, half):
+            if half == 0:
+                inv_p[i] = work.tile([P, N], F32, name="ee")
+            nc.scalar.activation(out=inv_p[i][:, half_cols(half)], in_=z[HEAD_P, i, half][:], func=ACT.Exp, scale=-1.0)
 
-        def b_exp(i, h):
-            if i >= NB:
-                return
-            if h == 0:
-                ee[i] = work.tile([P, N], F32, name="ee")
-            nc.scalar.activation(out=ee[i][:, NT * h:NT * (h + 1)], in_=z[0, i, h][:], func=ACT.Exp, scale=-1.0)
+        def tanh_z1(i, half):
+            z1_tanh[i, half] = work.tile([P, BANK], F32, name="tt")
+            nc.scalar.activation(out=z1_tanh[i, half][:], in_=z[HEAD_ERR, i, half][:], func=ACT.Tanh, scale=0.5)
 
-        def b_u(i, h):
-            uu[i, h] = psum.tile([P, NT], F32, name="up", bufs=UB)
-            nc.tensor.matmul(out=uu[i, h][:], lhsT=neg2[:], rhs=y_sb[i][:, NT * h:NT * (h + 1)], start=True, stop=False)
+        def diff_matmul(i, half):
+            diff[i, half] = psum.tile([P, BANK], F32, name="up")
+            nc.tensor.matmul(out=diff[i, half][:], lhsT=neg2[:], rhs=y_sb[i][:, half_cols(half)], start=True, stop=False)
             for c in range(4):
                 cols = slice(P * c, P * (c + 1))
-                nc.tensor.matmul(out=uu[i, h][:, cols], lhsT=tt[i, h][:, cols], rhs=ident[:], is_transpose=True, start=False, stop=(c == 3))
+                nc.tensor.matmul(
+                    out=diff[i, half][:, cols],
+                    lhsT=z1_tanh[i, half][:, cols],
+                    rhs=ident[:],
+                    is_transpose=True,
+                    start=False,
+                    stop=(c == 3),
+                )
 
-        def b_sq(i, h):
-            er[i, h] = work.tile([P, NT], F32, name="er", bufs=4)
-            nc.scalar.activation(out=er[i, h][:], in_=uu[i, h][:], func=ACT.Square, scale=0.5, bias=0.5)
+        def square(i, half):
+            err[i, half] = work.tile([P, BANK], F32, name="er", bufs=4)
+            nc.scalar.activation(out=err[i, half][:], in_=diff[i, half][:], func=ACT.Square, scale=0.5, bias=0.5)
 
-        def b_clamp(i):
-            nc.vector.tensor_scalar(out=ee[i][:], in0=ee[i][:], scalar1=4.0, scalar2=1.0, op0=ALU.min, op1=ALU.add)
+        def clamp(i):
+            nc.vector.tensor_scalar(out=inv_p[i][:], in0=inv_p[i][:], scalar1=4.0, scalar2=1.0, op0=ALU.min, op1=ALU.add)
 
-        def pool_share(i):
-            return N - GC0 * (i == 0) - GCUT * (i + 2 >= NB)
+        def gpsimd_cols(i):
+            return N - {0: FIRST_REST, TILES - 1: LAST_REST}.get(i, 0)
 
-        def pool_extra(i):
-            return GX if 0 < i < NB - 2 else 0
+        def weight_on_gpsimd(i):
+            weight[i] = work.tile([P, N], F32, name="ww")
+            cols = slice(0, gpsimd_cols(i))
+            nc.gpsimd.tensor_tensor(out=weight[i][:, cols], in0=inv_p[i][:, cols], in1=o_sb[i][:, cols], op=ALU.mult)
 
-        def g_wf(i):
-            if pool_extra(i):
-                c = slice(0, pool_extra(i))
-                nc.gpsimd.tensor_tensor(out=ff[i][:, c], in0=ww[i][:, c], in1=ff[i][:, c], op=ALU.mult)
+        def weight_rest(i):
+            if gpsimd_cols(i) < N:
+                cols = slice(gpsimd_cols(i), N)
+                nc.vector.tensor_tensor(out=weight[i][:, cols], in0=inv_p[i][:, cols], in1=o_sb[i][:, cols], op=ALU.mult)
 
-        def b_w(i):
-            ww[i] = work.tile([P, N], F32, name="ww", bufs=3)
-            c = slice(0, pool_share(i))
-            nc.gpsimd.tensor_tensor(out=ww[i][:, c], in0=ee[i][:, c], in1=o_sb[i][:, c], op=ALU.mult)
+        def err_minus_e(i, half):
+            if half == 0:
+                gap[i] = work.tile([P, N], F32, name="ff", bufs=2)
+            nc.vector.tensor_tensor(out=gap[i][:, half_cols(half)], in0=err[i, half][:], in1=z[HEAD_E, i, half][:], op=ALU.subtract)
 
-        def b_w_rest(i):
-            c = slice(pool_share(i), N)
-            if pool_share(i) < N:
-                nc.vector.tensor_tensor(out=ww[i][:, c], in0=ee[i][:, c], in1=o_sb[i][:, c], op=ALU.mult)
+        def weigh_gap(i, cols):
+            nc.vector.tensor_tensor(out=gap[i][:, cols], in0=weight[i][:, cols], in1=gap[i][:, cols], op=ALU.mult)
 
-        def b_f(i, h):
-            if h == 0:
-                ff[i] = work.tile([P, N], F32, name="ff", bufs=2)
-            nc.vector.tensor_tensor(out=ff[i][:, NT * h:NT * (h + 1)], in0=er[i, h][:], in1=z[2, i, h][:], op=ALU.subtract)
+        def sum_and_store(i, c0, width):
+            half, cols = c0 // BANK, slice(c0, c0 + width)
+            e = z[HEAD_E, i, half][:, c0 - BANK * half:c0 - BANK * half + width]
+            nc.vector.tensor_tensor(out=weight[i][:, cols], in0=e, in1=gap[i][:, cols], op=ALU.add)
+            nc.sync.dma_start(out=out[P * i:P * (i + 1), cols], in_=weight[i][:, cols])
 
-        def b_wf(i, cols):
-            nc.vector.tensor_tensor(out=ff[i][:, cols], in0=ww[i][:, cols], in1=ff[i][:, cols], op=ALU.mult)
-
-        def b_out(i, c0, width):
-            h = c0 // NT
-            nc.vector.tensor_tensor(out=ww[i][:, c0:c0 + width], in0=z[2, i, h][:, c0 - NT * h:c0 - NT * h + width], in1=ff[i][:, c0:c0 + width], op=ALU.add)
-            nc.sync.dma_start(out=out[P * i:P * (i + 1), c0:c0 + width], in_=ww[i][:, c0:c0 + width])
-
-
-        lo, hi, both = slice(0, NT), slice(NT, N), slice(0, N)
-        nc.tensor.matmul(out=g_ps[:], lhsT=ident_bf[:], rhs=g_bf[:].unsqueeze(1).to_broadcast([P, P, 4]), start=True, stop=True)
+        nc.tensor.matmul(
+            out=gain_ps[:], lhsT=ident_bf[:], rhs=gain[:].unsqueeze(1).to_broadcast([P, P, 4]), start=True, stop=True
+        )
         for j in (0, 2):
-            wh_widen(0, j, True)
-        for cols in (lo, hi):
+            widen_on_vector(HEAD_P, j, BOTH)
+        for cols in (LO, HI):
             for j in (1, 3):
-                wh_widen(0, j, False, cols)
-        wh_turn(0, 0)
-        wh_turn(0, 1)
-        x_trans(0)
-        wh_turn(0, 2)
-        for j in range(2):
-            wh_widen(1, j, True)
-        wh_widen(1, 2, True, lo)
-        wh_widen(1, 2, False, hi)
-        w_inter(0)
-        w_inter(1)
-        wh_widen(1, 3, False)
-        wh_copy(0, 0)
-        wh_turn(0, 3)
-        x_trans(1)
-        wh_copy(0, 1)
+                widen_on_scalar(HEAD_P, j, cols)
+        wh_turn(0)
+        wh_turn(1)
+        x_transpose(0)
+        wh_turn(2)
+        for j in (0, 1):
+            widen_on_vector(HEAD_ERR, j, BOTH)
+        widen_on_vector(HEAD_ERR, 2, LO)
+        widen_on_scalar(HEAD_ERR, 2, HI)
+        for c in range(PASSES):
+            w_interleave(c)
+        widen_on_scalar(HEAD_ERR, 3, BOTH)
+        wh_copy(0)
+        wh_turn(3)
+        x_transpose(1)
+        wh_copy(1)
         x_copy(0)
-        wh_inter(1, lo)
-        x_quant(0, 1)
-        w_quant()
-        wh_widen(2, 0, False)
-        wh_copy(0, 2)
-        wh_copy(0, 3)
+        wh_interleave(HEAD_ERR, LO)
+        x_quantize(0)
+        w_quantize()
+        widen_on_scalar(HEAD_E, 0, BOTH)
+        wh_copy(2)
+        wh_copy(3)
         h_matmul(0)
-        x_trans(2)
+        x_transpose(2)
         x_copy(1)
-        wh_inter(1, hi)
-        wh_quant(0, both)
-        x_quant(1, 1)
+        wh_interleave(HEAD_ERR, HI)
+        wh_quantize(HEAD_P, BOTH)
+        x_quantize(1)
         h_matmul(1)
-        wh_widen(2, 1, False)
-        h_tanh(0)
+        widen_on_scalar(HEAD_E, 1, BOTH)
+        h_activate(0)
         x_copy(2)
-        wh_quant(1, lo)
+        wh_quantize(HEAD_ERR, LO)
         h_gain(0)
-        wh_widen(2, 3, True)
-        h_quant(0)
-        wh_widen(2, 2, False)
-        z_matmul(0, 0, 0)
-        z_matmul(1, 0, 0)
-        h_tanh(1)
-        x_quant(2, 1)
-        wh_quant(1, hi)
+        widen_on_vector(HEAD_E, 3, BOTH)
+        h_quantize(0)
+        widen_on_scalar(HEAD_E, 2, BOTH)
+        z_matmul(HEAD_P, 0, 0)
+        z_matmul(HEAD_ERR, 0, 0)
+        h_activate(1)
+        x_quantize(2)
+        wh_quantize(HEAD_ERR, HI)
 
-        for k in range(NB):
-            b_exp(k, 0)
-            x_trans(k + 3)
+        for k in range(TILES):
+            exp_z0(k, 0)
+            x_transpose(k + 3)
             if k > 1:
-                b_out(k - 2, 0, NT)
-            b_tanh(k, 0)
-            z_matmul(0, k, 1)
+                sum_and_store(k - 2, 0, BANK)
+            tanh_z1(k, 0)
+            z_matmul(HEAD_P, k, 1)
             if k > 0:
-                z_matmul(2, k - 1, 1)
-                b_sq(k - 1, 1)
-            z_matmul(1, k, 1)
+                z_matmul(HEAD_E, k - 1, 1)
+                square(k - 1, 1)
+            z_matmul(HEAD_ERR, k, 1)
             if k > 1:
-                b_out(k - 2, NT, NT)
+                sum_and_store(k - 2, BANK, BANK)
             if k > 0:
-                z_matmul(2, k, 0)
+                z_matmul(HEAD_E, k, 0)
             if k != 1:
                 h_gain(k + 1)
             if k == 0:
-                wh_inter(2, lo)
+                wh_interleave(HEAD_E, LO)
             x_copy(k + 3)
-            b_u(k, 0)
-            b_exp(k, 1)
+            diff_matmul(k, 0)
+            exp_z0(k, 1)
             if k > 0:
-                b_f(k - 1, 1)
+                err_minus_e(k - 1, 1)
             h_matmul(k + 2)
-            b_tanh(k, 1)
+            tanh_z1(k, 1)
             if k > 0:
-                b_w_rest(k - 1)
-            h_quant(k + 1)
+                weight_rest(k - 1)
+            h_quantize(k + 1)
             if k == 0:
-                wh_inter(2, hi)
-            x_quant(k + 3, 1)
+                wh_interleave(HEAD_E, HI)
+            x_quantize(k + 3)
             if k == 0:
-                wh_quant(2, lo)
-            z_matmul(0, k + 1, 0)
-            b_sq(k, 0)
-            z_matmul(1, k + 1, 0)
-            b_clamp(k)
-            b_w(k)
+                wh_quantize(HEAD_E, LO)
+            z_matmul(HEAD_P, k + 1, 0)
+            square(k, 0)
+            z_matmul(HEAD_ERR, k + 1, 0)
+            clamp(k)
+            weight_on_gpsimd(k)
             if k > 0:
-                b_wf(k - 1, slice(pool_extra(k - 1), N))
-            h_tanh(k + 2)
-            b_u(k, 1)
+                weigh_gap(k - 1, BOTH)
+            h_activate(k + 2)
+            diff_matmul(k, 1)
             if k == 0:
-                wh_quant(2, hi)
-                z_matmul(2, 0, 0)
+                wh_quantize(HEAD_E, HI)
+                z_matmul(HEAD_E, 0, 0)
                 h_gain(2)
-            b_f(k, 0)
-            g_wf(k)
-        k = NB - 1
-        z_matmul(2, k, 1)
-        b_out(k - 1, 0, NT)
-        b_sq(k, 1)
-        b_out(k - 1, NT, NT)
-        b_f(k, 1)
-        b_w_rest(k)
-        b_wf(k, slice(0, NT))
-        b_wf(k, slice(NT, N))
-        b_out(k, 0, NT)
-        b_out(k, NT, NT - LASTW)
-        b_out(k, N - LASTW, LASTW)
+            err_minus_e(k, 0)
+
+        last = TILES - 1
+        z_matmul(HEAD_E, last, 1)
+        sum_and_store(last - 1, 0, BANK)
+        square(last, 1)
+        sum_and_store(last - 1, BANK, BANK)
+        err_minus_e(last, 1)
+        weight_rest(last)
+        weigh_gap(last, LO)
+        weigh_gap(last, HI)
+        sum_and_store(last, 0, BANK)
+        sum_and_store(last, BANK, BANK - LAST_STORE)
+        sum_and_store(last, N - LAST_STORE, LAST_STORE)

@@ -23,6 +23,7 @@ LO, HI, BOTH = slice(0, BANK), slice(BANK, N), slice(0, N)
 HEAD_P, HEAD_ERR, HEAD_E = 0, 1, 2
 
 E_BANKS = 3
+EARLY_X = 5
 FIRST_REST, LAST_REST = 256, 128
 LAST_STORE = 256
 
@@ -106,7 +107,7 @@ def tile_escmdoublyrobusterrormap_kernel(tc, x, w, g, wh_bytes, wh_scale, o, y, 
         def x_transpose(i):
             if i >= TILES:
                 return
-            if i < E_BANKS:
+            if i < EARLY_X:
                 x_t[i] = psum.tile([P, PASSES, 2, P], F32, name="xt", tag="z2", bufs=E_BANKS)
             else:
                 x_t[i] = psum.tile([P, PASSES, 2, P], F32, name="xt", tag="aux")
@@ -292,7 +293,7 @@ def tile_escmdoublyrobusterrormap_kernel(tc, x, w, g, wh_bytes, wh_scale, o, y, 
             return N - {0: FIRST_REST, TILES - 1: LAST_REST}.get(i, 0)
 
         def weight_on_gpsimd(i):
-            weight[i] = work.tile([P, N], F32, name="ww")
+            weight[i] = work.tile([P, N], F32, name="ww", bufs=TILES)
             cols = slice(0, gpsimd_cols(i))
             nc.gpsimd.tensor_tensor(out=weight[i][:, cols], in0=inv_p[i][:, cols], in1=o_sb[i][:, cols], op=ALU.mult)
 
@@ -327,16 +328,14 @@ def tile_escmdoublyrobusterrormap_kernel(tc, x, w, g, wh_bytes, wh_scale, o, y, 
         wh_turn(1)
         x_transpose(0)
         wh_turn(2)
-        for j in (0, 1):
+        for j in (0, 1, 2):
             widen_on_vector(HEAD_ERR, j, BOTH)
-        widen_on_vector(HEAD_ERR, 2, LO)
-        widen_on_scalar(HEAD_ERR, 2, HI)
         for c in range(PASSES):
             w_interleave(c)
         widen_on_scalar(HEAD_ERR, 3, BOTH)
         wh_copy(0)
-        wh_turn(3)
         x_transpose(1)
+        wh_turn(3)
         wh_copy(1)
         x_copy(0)
         wh_interleave(HEAD_ERR, LO)
@@ -344,53 +343,63 @@ def tile_escmdoublyrobusterrormap_kernel(tc, x, w, g, wh_bytes, wh_scale, o, y, 
         w_quantize()
         widen_on_scalar(HEAD_E, 0, BOTH)
         wh_copy(2)
-        wh_copy(3)
-        h_matmul(0)
-        x_transpose(2)
         x_copy(1)
+        wh_copy(3)
+        x_transpose(2)
+        h_matmul(0)
+        x_transpose(3)
         wh_interleave(HEAD_ERR, HI)
-        wh_quantize(HEAD_P, BOTH)
         x_quantize(1)
         h_matmul(1)
-        widen_on_scalar(HEAD_E, 1, BOTH)
-        h_activate(0)
         x_copy(2)
-        wh_quantize(HEAD_ERR, LO)
+        x_transpose(4)
+        h_activate(0)
+        wh_quantize(HEAD_P, BOTH)
+        x_quantize(2)
+        h_matmul(2)
+        widen_on_scalar(HEAD_E, 1, BOTH)
+        h_activate(1)
         h_gain(0)
-        widen_on_vector(HEAD_E, 3, BOTH)
+        wh_quantize(HEAD_ERR, LO)
         h_quantize(0)
+        widen_on_vector(HEAD_E, 3, LO)
         widen_on_scalar(HEAD_E, 2, BOTH)
         z_matmul(HEAD_P, 0, 0)
         z_matmul(HEAD_ERR, 0, 0)
-        h_activate(1)
-        x_quantize(2)
         wh_quantize(HEAD_ERR, HI)
 
         for k in range(TILES):
             exp_z0(k, 0)
-            x_transpose(k + 3)
+            if k > 1:
+                x_transpose(k + 3)
             if k > 1:
                 sum_and_store(k - 2, 0, BANK)
             tanh_z1(k, 0)
             z_matmul(HEAD_P, k, 1)
-            if k > 0:
+            if k > 1:
                 z_matmul(HEAD_E, k - 1, 1)
+            if k > 0:
                 square(k - 1, 1)
+            else:
+                widen_on_scalar(HEAD_E, 3, HI)
             z_matmul(HEAD_ERR, k, 1)
             if k > 1:
                 sum_and_store(k - 2, BANK, BANK)
-            if k > 0:
-                z_matmul(HEAD_E, k, 0)
             if k != 1:
                 h_gain(k + 1)
             if k == 0:
                 wh_interleave(HEAD_E, LO)
             x_copy(k + 3)
+            if k > 1:
+                z_matmul(HEAD_E, k, 0)
             diff_matmul(k, 0)
+            if k == 1:
+                z_matmul(HEAD_E, k, 0)
             exp_z0(k, 1)
             if k > 0:
                 err_minus_e(k - 1, 1)
-            h_matmul(k + 2)
+            if k > 0:
+                h_matmul(k + 2)
             tanh_z1(k, 1)
             if k > 0:
                 weight_rest(k - 1)
@@ -412,6 +421,7 @@ def tile_escmdoublyrobusterrormap_kernel(tc, x, w, g, wh_bytes, wh_scale, o, y, 
             if k == 0:
                 wh_quantize(HEAD_E, HI)
                 z_matmul(HEAD_E, 0, 0)
+                z_matmul(HEAD_E, 0, 1)
                 h_gain(2)
             err_minus_e(k, 0)
 
@@ -423,7 +433,8 @@ def tile_escmdoublyrobusterrormap_kernel(tc, x, w, g, wh_bytes, wh_scale, o, y, 
         err_minus_e(last, 1)
         weight_rest(last)
         weigh_gap(last, LO)
-        weigh_gap(last, HI)
+        weigh_gap(last, slice(BANK, N - LAST_STORE))
         sum_and_store(last, 0, BANK)
+        weigh_gap(last, slice(N - LAST_STORE, N))
         sum_and_store(last, BANK, BANK - LAST_STORE)
         sum_and_store(last, N - LAST_STORE, LAST_STORE)

@@ -47,24 +47,28 @@ def tile_escmdoublyrobusterrormap_kernel(tc, x, w, g, wh_bytes, wh_scale, o, y, 
             w_raw[c] = const.tile([P, 4, H], BF16, name="w_raw%d" % c)
             nc.sync.dma_start(out=w_raw[c][:], in_=w[512 * c:512 * (c + 1), :].rearrange("(p j) c -> p j c", j=4))
 
-        def load_wh(t, planes_per_dma):
-            wh_raw[t] = const.tile([P, 4, N], U8, name="wh_b%d" % t)
+        def load_wh(t, j):
+            if j == 0:
+                wh_raw[t] = const.tile([P, 4, N], U8, name="wh_b%d" % t)
             rows = wh_bytes[t].rearrange("(p j) n -> p j n", j=4)
-            for j in range(0, 4, planes_per_dma):
-                nc.sync.dma_start(out=wh_raw[t][:, j:j + planes_per_dma, :], in_=rows[:, j:j + planes_per_dma, :])
+            nc.sync.dma_start(out=wh_raw[t][:, j:j + 2, :], in_=rows[:, j:j + 2, :])
 
         def load_rows(tiles, src, label, i):
             tiles[i] = const.tile([P, N], BF16, name="%s_%d" % (label, i))
             nc.sync.dma_start(out=tiles[i][:], in_=src[P * i:P * (i + 1), :])
 
+        load_wh(HEAD_P, 0)
         load_wh(HEAD_P, 2)
+        load_wh(HEAD_ERR, 0)
         load_wh(HEAD_ERR, 2)
         load_w(0)
-        load_w(1)
         load_rows(x_sb, x, "x", 0)
-        load_wh(HEAD_E, 4)
-        for i in range(1, 4):
-            load_rows(x_sb, x, "x", i)
+        load_w(1)
+        load_wh(HEAD_E, 0)
+        load_rows(x_sb, x, "x", 1)
+        load_wh(HEAD_E, 2)
+        load_rows(x_sb, x, "x", 2)
+        load_rows(x_sb, x, "x", 3)
         for i in range(TILES):
             load_rows(y_sb, y, "y", i)
             load_rows(o_sb, o, "o", i)
@@ -169,10 +173,12 @@ def tile_escmdoublyrobusterrormap_kernel(tc, x, w, g, wh_bytes, wh_scale, o, y, 
                 out=h_q[:, i, :].bitcast(FP8X4), scales=h_s[:, i, :], in_=h_g[i][:].rearrange("p r s -> p (r s)")
             )
 
-        def wide_tile(t):
-            if t not in wh_wide:
-                wh_wide[t] = const.tile([P, 4, N], BF16, name="wh_p%d" % t)
-            return wh_wide[t]
+        def wide(t, cols):
+            width = BANK
+            part = cols.start // width
+            if (t, part) not in wh_wide:
+                wh_wide[t, part] = const.tile([P, 4, width], BF16, name="wh_p%d%d" % (t, part))
+            return wh_wide[t, part][:, :, cols.start - width * part:cols.stop - width * part]
 
         def grouped_tile(t):
             if t not in wh_g:
@@ -181,7 +187,7 @@ def tile_escmdoublyrobusterrormap_kernel(tc, x, w, g, wh_bytes, wh_scale, o, y, 
 
         def widen_on_vector(t, j, cols):
             nc.vector.tensor_scalar(
-                out=wide_tile(t)[:, j, cols],
+                out=wide(t, cols)[:, j, :],
                 in0=wh_raw[t][:, j, cols].bitcast(FP8),
                 scalar1=scale[:, j:j + 1],
                 scalar2=None,
@@ -190,13 +196,13 @@ def tile_escmdoublyrobusterrormap_kernel(tc, x, w, g, wh_bytes, wh_scale, o, y, 
 
         def widen_on_scalar(t, j, cols):
             nc.scalar.activation(
-                out=wide_tile(t)[:, j, cols], in_=wh_raw[t][:, j, cols].bitcast(FP8), func=ACT.Copy, scale=scale[:, j:j + 1]
+                out=wide(t, cols)[:, j, :], in_=wh_raw[t][:, j, cols].bitcast(FP8), func=ACT.Copy, scale=scale[:, j:j + 1]
             )
 
         def wh_interleave(t, cols):
             nc.vector.tensor_copy(
                 out=grouped_tile(t)[:, cols, :].rearrange("p (c i) j -> p c j i", i=4),
-                in_=wh_wide[t][:, :, cols].rearrange("p j (c i) -> p c j i", i=4),
+                in_=wide(t, cols).rearrange("p j (c i) -> p c j i", i=4),
             )
 
         def wh_turn(quarter):
@@ -206,15 +212,15 @@ def tile_escmdoublyrobusterrormap_kernel(tc, x, w, g, wh_bytes, wh_scale, o, y, 
                 nc.tensor.matmul(
                     out=wh_ps[quarter][:, b, :, :].rearrange("p n j -> p (n j)"),
                     lhsT=ident_bf[:],
-                    rhs=wh_wide[HEAD_P][:, :, c0:c0 + P].rearrange("p j n -> p n j"),
+                    rhs=wide(HEAD_P, slice(c0, c0 + P)).rearrange("p j n -> p n j"),
                     start=True,
                     stop=True,
                 )
 
         def wh_copy(quarter):
             nc.scalar.copy(
-                out=grouped_tile(HEAD_P)[:, 2 * P * quarter:2 * P * (quarter + 1), :].rearrange("p n j -> p (n j)"),
-                in_=wh_ps[quarter][:].rearrange("p b n j -> p (b n j)"),
+                out=grouped_tile(HEAD_P)[:, 2 * P * quarter:2 * P * (quarter + 1), :].rearrange("p n j -> p (n j)").bitcast(F32),
+                in_=wh_ps[quarter][:].rearrange("p b n j -> p (b n j)").bitcast(F32),
             )
 
         def wh_quantize(t, cols):
@@ -319,54 +325,66 @@ def tile_escmdoublyrobusterrormap_kernel(tc, x, w, g, wh_bytes, wh_scale, o, y, 
         nc.tensor.matmul(
             out=gain_ps[:], lhsT=ident_bf[:], rhs=gain[:].unsqueeze(1).to_broadcast([P, P, 4]), start=True, stop=True
         )
-        for j in (0, 2):
-            widen_on_vector(HEAD_P, j, BOTH)
-        for cols in (LO, HI):
-            for j in (1, 3):
-                widen_on_scalar(HEAD_P, j, cols)
+        widen_on_vector(HEAD_P,0,LO)
+        widen_on_scalar(HEAD_P,1,LO)
+        widen_on_vector(HEAD_P,0,HI)
+        widen_on_vector(HEAD_P,2,LO)
+        widen_on_scalar(HEAD_P,3,LO)
+        widen_on_vector(HEAD_P,2,HI)
         wh_turn(0)
         wh_turn(1)
+        widen_on_vector(HEAD_ERR,0,LO)
+        widen_on_vector(HEAD_P,1,HI)
+        widen_on_scalar(HEAD_ERR,1,LO)
+        widen_on_vector(HEAD_ERR,2,LO)
+        widen_on_scalar(HEAD_ERR,3,LO)
+        widen_on_vector(HEAD_P,3,HI)
+        widen_on_vector(HEAD_ERR,0,HI)
+        wh_interleave(HEAD_ERR,LO)
+        w_interleave(0)
+        w_interleave(1)
+        widen_on_scalar(HEAD_ERR,1,HI)
+        widen_on_scalar(HEAD_ERR,2,HI)
+        wh_copy(0)
+        widen_on_scalar(HEAD_ERR,3,HI)
         x_transpose(0)
         wh_turn(2)
-        for j in (0, 1, 2):
-            widen_on_vector(HEAD_ERR, j, BOTH)
-        for c in range(PASSES):
-            w_interleave(c)
-        widen_on_scalar(HEAD_ERR, 3, BOTH)
-        wh_copy(0)
         x_transpose(1)
         wh_turn(3)
         wh_copy(1)
         x_copy(0)
-        wh_interleave(HEAD_ERR, LO)
         x_quantize(0)
         w_quantize()
-        widen_on_scalar(HEAD_E, 0, BOTH)
+        widen_on_scalar(HEAD_E,0,LO)
+        widen_on_scalar(HEAD_E,1,LO)
         wh_copy(2)
         x_copy(1)
-        wh_copy(3)
-        x_transpose(2)
+        widen_on_scalar(HEAD_E,2,LO)
+        widen_on_scalar(HEAD_E,3,LO)
         h_matmul(0)
-        x_transpose(3)
-        wh_interleave(HEAD_ERR, HI)
+        h_activate(0)
+        x_transpose(2)
+        wh_copy(3)
+        x_copy(2)
+        wh_interleave(HEAD_ERR,HI)
         x_quantize(1)
         h_matmul(1)
-        x_copy(2)
+        x_transpose(3)
         x_transpose(4)
-        h_activate(0)
-        wh_quantize(HEAD_P, BOTH)
-        x_quantize(2)
-        h_matmul(2)
-        widen_on_scalar(HEAD_E, 1, BOTH)
-        h_activate(1)
+        wh_quantize(HEAD_ERR,LO)
+        wh_quantize(HEAD_P,LO)
         h_gain(0)
-        wh_quantize(HEAD_ERR, LO)
+        wh_quantize(HEAD_P,HI)
         h_quantize(0)
-        widen_on_vector(HEAD_E, 3, LO)
-        widen_on_scalar(HEAD_E, 2, BOTH)
-        z_matmul(HEAD_P, 0, 0)
-        z_matmul(HEAD_ERR, 0, 0)
-        wh_quantize(HEAD_ERR, HI)
+        x_quantize(2)
+        h_activate(1)
+        widen_on_scalar(HEAD_E,0,HI)
+        widen_on_scalar(HEAD_E,1,HI)
+        widen_on_scalar(HEAD_E,2,HI)
+        z_matmul(HEAD_P, 0,0)
+        z_matmul(HEAD_ERR, 0,0)
+        h_matmul(2)
+        wh_quantize(HEAD_ERR,HI)
 
         for k in range(TILES):
             exp_z0(k, 0)
@@ -374,13 +392,14 @@ def tile_escmdoublyrobusterrormap_kernel(tc, x, w, g, wh_bytes, wh_scale, o, y, 
                 x_transpose(k + 3)
             if k > 1:
                 sum_and_store(k - 2, 0, BANK)
+            if k == 1:
+                square(k - 1, 1)
             tanh_z1(k, 0)
             z_matmul(HEAD_P, k, 1)
             if k > 1:
                 z_matmul(HEAD_E, k - 1, 1)
-            if k > 0:
                 square(k - 1, 1)
-            else:
+            if k == 0:
                 widen_on_scalar(HEAD_E, 3, HI)
             z_matmul(HEAD_ERR, k, 1)
             if k > 1:
@@ -389,13 +408,15 @@ def tile_escmdoublyrobusterrormap_kernel(tc, x, w, g, wh_bytes, wh_scale, o, y, 
                 h_gain(k + 1)
             if k == 0:
                 wh_interleave(HEAD_E, LO)
-            x_copy(k + 3)
+            if k != 1:
+                x_copy(k + 3)
             if k > 1:
                 z_matmul(HEAD_E, k, 0)
             diff_matmul(k, 0)
-            if k == 1:
-                z_matmul(HEAD_E, k, 0)
             exp_z0(k, 1)
+            if k == 1:
+                x_copy(k + 3)
+                z_matmul(HEAD_E, k, 0)
             if k > 0:
                 err_minus_e(k - 1, 1)
             if k > 0:
@@ -405,15 +426,17 @@ def tile_escmdoublyrobusterrormap_kernel(tc, x, w, g, wh_bytes, wh_scale, o, y, 
                 weight_rest(k - 1)
             h_quantize(k + 1)
             if k == 0:
-                wh_interleave(HEAD_E, HI)
-            x_quantize(k + 3)
-            if k == 0:
                 wh_quantize(HEAD_E, LO)
+                wh_interleave(HEAD_E, HI)
+            if k != 1:
+                x_quantize(k + 3)
             z_matmul(HEAD_P, k + 1, 0)
             square(k, 0)
             z_matmul(HEAD_ERR, k + 1, 0)
             clamp(k)
             weight_on_gpsimd(k)
+            if k == 1:
+                x_quantize(k + 3)
             if k > 0:
                 weigh_gap(k - 1, BOTH)
             h_activate(k + 2)

@@ -408,15 +408,13 @@ def tile_escmdoublyrobusterrormap_kernel(tc, x, w, g, wh_bytes, wh_scale, o, y, 
                 h_gain(k + 1)
             if k == 0:
                 wh_interleave(HEAD_E, LO)
-            if k != 1:
-                x_copy(k + 3)
+            x_copy(k + 3)
             if k > 1:
                 z_matmul(HEAD_E, k, 0)
             diff_matmul(k, 0)
-            exp_z0(k, 1)
             if k == 1:
-                x_copy(k + 3)
                 z_matmul(HEAD_E, k, 0)
+            exp_z0(k, 1)
             if k > 0:
                 err_minus_e(k - 1, 1)
             if k > 0:
@@ -428,15 +426,12 @@ def tile_escmdoublyrobusterrormap_kernel(tc, x, w, g, wh_bytes, wh_scale, o, y, 
             if k == 0:
                 wh_quantize(HEAD_E, LO)
                 wh_interleave(HEAD_E, HI)
-            if k != 1:
-                x_quantize(k + 3)
+            x_quantize(k + 3)
             z_matmul(HEAD_P, k + 1, 0)
             square(k, 0)
             z_matmul(HEAD_ERR, k + 1, 0)
             clamp(k)
             weight_on_gpsimd(k)
-            if k == 1:
-                x_quantize(k + 3)
             if k > 0:
                 weigh_gap(k - 1, BOTH)
             h_activate(k + 2)

@@ -231,18 +231,21 @@ def tile_escmdoublyrobusterrormap_kernel(tc, x, w, g, wh_bytes, wh_scale, o, y, 
             )
 
         z, z1_tanh, inv_p, diff, err, weight, gap = {}, {}, {}, {}, {}, {}, {}
+        neg_e, gap_ps = {}, {}
 
         def half_cols(half):
             return (LO, HI)[half]
 
-        def z_matmul(t, i, half):
+        def z_matmul(t, i, half, bank=None, turned=None):
             if i >= TILES:
                 return
-            if t == HEAD_E and half == 1 and i >= TILES - 2:
-                z[t, i, half] = psum.tile([P, BANK], F32, name="z_late", tag="aux" if i == TILES - 2 else "g_ps")
+            if turned is None:
+                turned = t == HEAD_ERR
+            if bank:
+                z[t, i, half] = psum.tile([P, BANK], F32, name="z_late", tag=bank)
             else:
                 z[t, i, half] = psum.tile([P, BANK], F32, name="z%d" % t, bufs=E_BANKS if t == HEAD_E else 1)
-            if t == HEAD_ERR:
+            if turned:
                 for c in range(4):
                     cols = slice(BANK * half + P * c, BANK * half + P * (c + 1))
                     nc.tensor.matmul_mx(
@@ -287,6 +290,36 @@ def tile_escmdoublyrobusterrormap_kernel(tc, x, w, g, wh_bytes, wh_scale, o, y, 
                     start=False,
                     stop=(c == 3),
                 )
+
+        def add_turned(bank, src, start, stop):
+            for c in range(4):
+                cols = slice(P * c, P * (c + 1))
+                nc.tensor.matmul(
+                    out=bank[:, cols], lhsT=src[:, cols], rhs=ident[:], is_transpose=True,
+                    start=(start and c == 0), stop=(stop and c == 3),
+                )
+
+        def diff_turned(i, half):
+            diff[i, half] = psum.tile([P, BANK], F32, name="up")
+            for c in range(4):
+                cols = slice(BANK * half + P * c, BANK * half + P * (c + 1))
+                nc.tensor.matmul(
+                    out=diff[i, half][:, P * c:P * (c + 1)], lhsT=y_sb[i][:, cols], rhs=neg2[:], start=(c == 0), stop=False
+                )
+            add_turned(diff[i, half], z1_tanh[i, half], False, True)
+
+        def minus_e(i, half):
+            neg_e[i, half] = work.tile([P, BANK], F32, name="tt")
+            nc.scalar.activation(out=neg_e[i, half][:], in_=z[HEAD_E, i, half][:], func=ACT.Copy, scale=-1.0)
+
+        def gap_matmul(i, half, bank):
+            gap_ps[i, half] = psum.tile([P, BANK], F32, name="gap_ps", tag=bank)
+            add_turned(gap_ps[i, half], neg_e[i, half], True, False)
+            add_turned(gap_ps[i, half], err[i, half], False, True)
+
+        def weigh_gap_from_psum(i, half):
+            cols = half_cols(half)
+            nc.vector.tensor_tensor(out=gap[i][:, cols], in0=weight[i][:, cols], in1=gap_ps[i, half][:], op=ALU.mult)
 
         def square(i, half):
             err[i, half] = work.tile([P, BANK], F32, name="er", bufs=4)
@@ -361,10 +394,11 @@ def tile_escmdoublyrobusterrormap_kernel(tc, x, w, g, wh_bytes, wh_scale, o, y, 
         x_copy(1)
         widen_on_scalar(HEAD_E,2,LO)
         widen_on_scalar(HEAD_E,3,LO)
+        wh_copy(3)
         h_matmul(0)
         h_activate(0)
         x_transpose(2)
-        wh_copy(3)
+        widen_on_scalar(HEAD_E,0,HI)
         x_copy(2)
         wh_interleave(HEAD_ERR,HI)
         x_quantize(1)
@@ -376,28 +410,26 @@ def tile_escmdoublyrobusterrormap_kernel(tc, x, w, g, wh_bytes, wh_scale, o, y, 
         h_gain(0)
         wh_quantize(HEAD_P,HI)
         h_quantize(0)
-        x_quantize(2)
         h_activate(1)
-        widen_on_scalar(HEAD_E,0,HI)
         widen_on_scalar(HEAD_E,1,HI)
         widen_on_scalar(HEAD_E,2,HI)
         z_matmul(HEAD_P, 0,0)
         z_matmul(HEAD_ERR, 0,0)
-        h_matmul(2)
         wh_quantize(HEAD_ERR,HI)
 
-        for k in range(TILES):
+        for k in range(TILES - 3):
             exp_z0(k, 0)
             if k > 1:
                 x_transpose(k + 3)
             if k > 1:
                 sum_and_store(k - 2, 0, BANK)
-            if k == 1:
+            if 0 < k <= 1:
                 square(k - 1, 1)
             tanh_z1(k, 0)
             z_matmul(HEAD_P, k, 1)
             if k > 1:
                 z_matmul(HEAD_E, k - 1, 1)
+            if k > 1:
                 square(k - 1, 1)
             if k == 0:
                 widen_on_scalar(HEAD_E, 3, HI)
@@ -424,35 +456,110 @@ def tile_escmdoublyrobusterrormap_kernel(tc, x, w, g, wh_bytes, wh_scale, o, y, 
                 weight_rest(k - 1)
             h_quantize(k + 1)
             if k == 0:
+                x_quantize(2)
+                h_matmul(2)
                 wh_quantize(HEAD_E, LO)
                 wh_interleave(HEAD_E, HI)
             x_quantize(k + 3)
             z_matmul(HEAD_P, k + 1, 0)
             square(k, 0)
             z_matmul(HEAD_ERR, k + 1, 0)
+            if 0 < k <= 0:
+                weigh_gap(k - 1, BOTH)
             clamp(k)
             weight_on_gpsimd(k)
             if k > 0:
                 weigh_gap(k - 1, BOTH)
             h_activate(k + 2)
+            if k == 0:
+                z_matmul(HEAD_E, 0, 0)
             diff_matmul(k, 1)
             if k == 0:
                 wh_quantize(HEAD_E, HI)
-                z_matmul(HEAD_E, 0, 0)
                 z_matmul(HEAD_E, 0, 1)
-                h_gain(2)
             err_minus_e(k, 0)
+            if k == 0:
+                h_gain(2)
 
-        last = TILES - 1
-        z_matmul(HEAD_E, last, 1)
-        sum_and_store(last - 1, 0, BANK)
-        square(last, 1)
-        sum_and_store(last - 1, BANK, BANK)
-        err_minus_e(last, 1)
-        weight_rest(last)
-        weigh_gap(last, LO)
-        weigh_gap(last, slice(BANK, N - LAST_STORE))
-        sum_and_store(last, 0, BANK)
-        weigh_gap(last, slice(N - LAST_STORE, N))
-        sum_and_store(last, BANK, BANK - LAST_STORE)
-        sum_and_store(last, N - LAST_STORE, LAST_STORE)
+        h_matmul(7)
+        exp_z0(5,0)
+        sum_and_store(3, 0, BANK)
+        tanh_z1(5,0)
+        z_matmul(HEAD_P, 5,1)
+        z_matmul(HEAD_ERR, 5,1,None,False)
+        z_matmul(HEAD_E, 4,1)
+        square(4,1)
+        sum_and_store(3, BANK, BANK)
+        h_gain(6)
+        diff_matmul(5,0)
+        h_activate(7)
+        exp_z0(5,1)
+        err_minus_e(4,1)
+        tanh_z1(5,1)
+        z_matmul(HEAD_E, 5,1,"aux",True)
+        h_quantize(6)
+        z_matmul(HEAD_P, 6,0)
+        z_matmul(HEAD_E, 5,0)
+        square(5,0)
+        z_matmul(HEAD_ERR, 6,0)
+        diff_turned(5,1)
+        clamp(5)
+        weight_on_gpsimd(5)
+        weigh_gap(4,BOTH)
+        minus_e(5,1)
+        err_minus_e(5,0)
+        exp_z0(6,0)
+        sum_and_store(4, 0, BANK)
+        tanh_z1(6,0)
+        z_matmul(HEAD_P, 6,1)
+        square(5,1)
+        z_matmul(HEAD_ERR, 6,1)
+        z_matmul(HEAD_E, 6,0)
+        h_gain(7)
+        sum_and_store(4, BANK, BANK)
+        diff_matmul(6,0)
+        gap_matmul(5,1,"g_ps")
+        exp_z0(6,1)
+        tanh_z1(6,1)
+        h_quantize(7)
+        z_matmul(HEAD_P, 7,0)
+        square(6,0)
+        z_matmul(HEAD_ERR, 7,0)
+        diff_matmul(6,1)
+        z_matmul(HEAD_E, 5,1)
+        clamp(6)
+        weight_on_gpsimd(6)
+        weigh_gap(5,LO)
+        err_minus_e(6,0)
+        exp_z0(7,0)
+        weigh_gap_from_psum(5,1)
+        sum_and_store(5, 0, BANK)
+        tanh_z1(7,0)
+        z_matmul(HEAD_P, 7,1)
+        z_matmul(HEAD_E, 6,1,"aux")
+        square(6,1)
+        z_matmul(HEAD_ERR, 7,1)
+        diff_matmul(7,0)
+        sum_and_store(5, BANK, BANK)
+        z_matmul(HEAD_E, 7,0)
+        exp_z0(7,1)
+        err_minus_e(6,1)
+        tanh_z1(7,1)
+        square(7,0)
+        clamp(7)
+        weight_on_gpsimd(7)
+        weigh_gap(6,BOTH)
+        diff_matmul(7,1)
+        err_minus_e(7,0)
+        z_matmul(HEAD_E, 7,1,"g_ps")
+        sum_and_store(6, 0, BANK)
+        square(7,1)
+        sum_and_store(6, BANK, BANK)
+        err_minus_e(7,1)
+        weight_rest(7)
+        weigh_gap(7,LO)
+        weigh_gap(7,slice(BANK,N-LAST_STORE))
+        sum_and_store(7, 0, BANK)
+        weigh_gap(7,slice(N-LAST_STORE,N))
+        sum_and_store(7,BANK,BANK-LAST_STORE)
+        sum_and_store(7,N-LAST_STORE,LAST_STORE)

from contextlib import ExitStack

import concourse.mybir as mybir
from concourse.masks import make_identity

B, D, H, N, T = 1024, 1024, 512, 1024, 3
FLOPS = 2 * B * D * H + 2 * T * B * H * N

F32 = mybir.dt.float32
BF16 = mybir.dt.bfloat16
U32 = mybir.dt.uint32
U8 = mybir.dt.uint8
FP8X4 = mybir.dt.float8_e4m3fn_x4
FP8 = mybir.dt.float8_e4m3fn
ACT = mybir.ActivationFunctionType
ALU = mybir.AluOpType

P = 128
BANK = 512
TILES = B // P
PASSES = D // 512
LO, HI, BOTH = slice(0, BANK), slice(BANK, N), slice(0, N)
HEAD_P, HEAD_ERR, HEAD_E = 0, 1, 2

E_BANKS = 3
EARLY_X = 5
FIRST_REST, LAST_REST = 256, 128
LAST_STORE = 256


def tile_escmdoublyrobusterrormap_kernel(tc, x, w, g, wh_bytes, wh_scale, o, y, out):
    nc = tc.nc
    with ExitStack() as ctx:
        const = ctx.enter_context(tc.tile_pool(name="const", bufs=1))
        work = ctx.enter_context(tc.tile_pool(name="work", bufs=3))
        psum = ctx.enter_context(tc.psum_pool(name="psum", bufs=1))
        ctx.enter_context(tc.manual_schedule())

        scale = const.tile([P, 4], F32, name="s_sb")
        nc.scalar.dma_start(out=scale[:], in_=wh_scale.rearrange("o (p j) q -> p (o j q)", j=4))
        gain = const.tile([P, 4], BF16, name="g_bf")
        nc.scalar.dma_start(out=gain[:], in_=g.rearrange("(p j) -> p j", j=4))

        w_raw, wh_raw, x_sb, o_sb, y_sb = {}, {}, {}, {}, {}

        def load_w(c):
            w_raw[c] = const.tile([P, 4, H], BF16, name="w_raw%d" % c)
            nc.sync.dma_start(out=w_raw[c][:], in_=w[512 * c:512 * (c + 1), :].rearrange("(p j) c -> p j c", j=4))

        def load_wh(t, j):
            if j == 0:
                wh_raw[t] = const.tile([P, 4, N], U8, name="wh_b%d" % t)
            rows = wh_bytes[t].rearrange("(p j) n -> p j n", j=4)
            nc.sync.dma_start(out=wh_raw[t][:, j:j + 2, :], in_=rows[:, j:j + 2, :])

        def load_rows(tiles, src, label, i):
            tiles[i] = const.tile([P, N], BF16, name="%s_%d" % (label, i))
            nc.sync.dma_start(out=tiles[i][:], in_=src[P * i:P * (i + 1), :])

        load_wh(HEAD_P, 0)
        load_wh(HEAD_P, 2)
        load_wh(HEAD_ERR, 0)
        load_wh(HEAD_ERR, 2)
        load_w(0)
        load_rows(x_sb, x, "x", 0)
        load_w(1)
        load_wh(HEAD_E, 0)
        load_rows(x_sb, x, "x", 1)
        load_wh(HEAD_E, 2)
        load_rows(x_sb, x, "x", 2)
        load_rows(x_sb, x, "x", 3)
        for i in range(TILES):
            load_rows(y_sb, y, "y", i)
            load_rows(o_sb, o, "o", i)
            if i + 4 < TILES:
                load_rows(x_sb, x, "x", i + 4)

        ident = const.tile([P, P], F32, name="ident")
        make_identity(nc, ident[:])
        neg2 = const.tile([P, P], BF16, name="neg2")
        nc.scalar.activation(out=neg2[:], in_=ident[:], func=ACT.Copy, scale=-2.0)
        ident_bf = const.tile([P, P], BF16, name="ident_bf")
        nc.gpsimd.tensor_scalar(out=ident_bf[:], in0=ident[:], scalar1=1.0, scalar2=0.0, op0=ALU.mult, op1=ALU.add)
        gain_ps = psum.tile([P, P, 4], F32, name="g_ps")

        w_g = const.tile([P, PASSES, 4 * H], BF16, align_bytes=64, name="w_g")
        w_q = const.tile([P, PASSES, H], U32, align_bytes=64, name="w_q")
        w_s = const.tile([P, PASSES, H], U8, align_bytes=64, name="w_s")
        x_q = const.tile([P, TILES, PASSES, P], U32, align_bytes=64, name="x_q")
        x_s = const.tile([P, TILES, PASSES, P], U8, align_bytes=64, name="x_s")
        wh_q = const.tile([P, T, N], U32, align_bytes=64, name="wh_q")
        wh_s = const.tile([P, T, N], U8, align_bytes=64, name="wh_s")
        h_q = const.tile([P, TILES, P], U32, align_bytes=64, name="h_q")
        h_s = const.tile([P, TILES, P], U8, align_bytes=64, name="h_s")
        x_t, x_g, h_pre, h_tanh, h_g = {}, {}, {}, {}, {}
        wh_wide, wh_ps, wh_g = {}, {}, {}

        def w_interleave(c):
            src = w_raw[c][:].rearrange("p j (a b u v) -> p u a j b v", b=2, u=2, v=2)
            dst = w_g[:, c, :].rearrange("p (u v a b j) -> p u a j b v", u=2, v=2, b=2, j=4)
            for u in range(2):
                nc.vector.tensor_copy(out=dst[:, u], in_=src[:, u])

        def w_quantize():
            nc.vector.quantize_mx(
                out=w_q[:].rearrange("p c n -> p (c n)").bitcast(FP8X4),
                scales=w_s[:].rearrange("p c n -> p (c n)"),
                in_=w_g[:].rearrange("p c n -> p (c n)"),
            )

        def x_transpose(i):
            if i >= TILES:
                return
            if i < EARLY_X:
                x_t[i] = psum.tile([P, PASSES, 2, P], F32, name="xt", tag="z2", bufs=E_BANKS)
            else:
                x_t[i] = psum.tile([P, PASSES, 2, P], F32, name="xt", tag="aux")
            words = x_sb[i][:].bitcast(F32)
            for c in range(PASSES):
                for u in range(2):
                    nc.tensor.transpose(x_t[i][:, c, u, :], words[:, 256 * c + u:256 * (c + 1):2], ident[:])

        def x_copy(i):
            if i >= TILES:
                return
            x_g[i] = work.tile([P, PASSES * P * 4], BF16, name="x_g", align_bytes=64)
            nc.scalar.copy(
                out=x_g[i][:].bitcast(F32).rearrange("p (c r u) -> p c r u", c=PASSES, u=2),
                in_=x_t[i][:].rearrange("p c u r -> p c r u"),
            )

        def x_quantize(i):
            if i >= TILES:
                return
            nc.vector.quantize_mx(
                out=x_q[:, i, :, :].rearrange("p c r -> p (c r)").bitcast(FP8X4),
                scales=x_s[:, i, :, :].rearrange("p c r -> p (c r)"),
                in_=x_g[i][:],
            )

        def h_matmul(i):
            if i >= TILES:
                return
            h_pre[i] = psum.tile([P, 4, P], F32, name="ht", tag="up" if i == 1 else "aux")
            for s in range(4):
                for c in range(PASSES):
                    nc.tensor.matmul_mx(
                        out=h_pre[i][:, s, :],
                        lhsT=w_q[:, c, P * s:P * (s + 1)].bitcast(FP8X4),
                        lhsT_scale=w_s[:, c, P * s:P * (s + 1)],
                        rhs=x_q[:, i, c, :].bitcast(FP8X4),
                        rhs_scale=x_s[:, i, c, :],
                        start=(c == 0),
                        stop=(c == PASSES - 1),
                    )

        def h_activate(i):
            if i >= TILES:
                return
            h_tanh[i] = work.tile([P, P, 4], F32, name="th")
            nc.scalar.activation(out=h_tanh[i][:], in_=h_pre[i][:].rearrange("p s r -> p r s"), func=ACT.Tanh)

        def h_gain(i):
            if i >= TILES:
                return
            h_g[i] = work.tile([P, P, 4], BF16, name="hg", align_bytes=64)
            nc.vector.tensor_tensor(out=h_g[i][:], in0=h_tanh[i][:], in1=gain_ps[:], op=ALU.mult)

        def h_quantize(i):
            if i >= TILES:
                return
            nc.vector.quantize_mx(
                out=h_q[:, i, :].bitcast(FP8X4), scales=h_s[:, i, :], in_=h_g[i][:].rearrange("p r s -> p (r s)")
            )

        def wide(t, cols):
            width = BANK
            part = cols.start // width
            if (t, part) not in wh_wide:
                wh_wide[t, part] = const.tile([P, 4, width], BF16, name="wh_p%d%d" % (t, part))
            return wh_wide[t, part][:, :, cols.start - width * part:cols.stop - width * part]

        def grouped_tile(t):
            if t not in wh_g:
                wh_g[t] = work.tile([P, N, 4], BF16, name="wh_g", align_bytes=64, bufs=2)
            return wh_g[t]

        def widen_on_vector(t, j, cols):
            nc.vector.tensor_scalar(
                out=wide(t, cols)[:, j, :],
                in0=wh_raw[t][:, j, cols].bitcast(FP8),
                scalar1=scale[:, j:j + 1],
                scalar2=None,
                op0=ALU.mult,
            )

        def widen_on_scalar(t, j, cols):
            nc.scalar.activation(
                out=wide(t, cols)[:, j, :], in_=wh_raw[t][:, j, cols].bitcast(FP8), func=ACT.Copy, scale=scale[:, j:j + 1]
            )

        def wh_interleave(t, cols):
            nc.vector.tensor_copy(
                out=grouped_tile(t)[:, cols, :].rearrange("p (c i) j -> p c j i", i=4),
                in_=wide(t, cols).rearrange("p j (c i) -> p c j i", i=4),
            )

        def wh_turn(quarter):
            wh_ps[quarter] = psum.tile([P, 2, P, 4], BF16, name="wh_ps", tag=("z0", "z1", "up")[quarter % 3])
            for b in range(2):
                c0 = 2 * P * quarter + P * b
                nc.tensor.matmul(
                    out=wh_ps[quarter][:, b, :, :].rearrange("p n j -> p (n j)"),
                    lhsT=ident_bf[:],
                    rhs=wide(HEAD_P, slice(c0, c0 + P)).rearrange("p j n -> p n j"),
                    start=True,
                    stop=True,
                )

        def wh_copy(quarter):
            nc.scalar.copy(
                out=grouped_tile(HEAD_P)[:, 2 * P * quarter:2 * P * (quarter + 1), :].rearrange("p n j -> p (n j)").bitcast(F32),
                in_=wh_ps[quarter][:].rearrange("p b n j -> p (b n j)").bitcast(F32),
            )

        def wh_quantize(t, cols):
            nc.vector.quantize_mx(
                out=wh_q[:, t, cols].bitcast(FP8X4),
                scales=wh_s[:, t, cols],
                in_=wh_g[t][:, cols, :].rearrange("p n j -> p (n j)"),
            )

        z, z1_tanh, inv_p, diff, err, weight, gap = {}, {}, {}, {}, {}, {}, {}
        neg_e, gap_ps = {}, {}

        def half_cols(half):
            return (LO, HI)[half]

        def z_matmul(t, i, half, bank=None, turned=None):
            if i >= TILES:
                return
            if turned is None:
                turned = t == HEAD_ERR
            if bank:
                z[t, i, half] = psum.tile([P, BANK], F32, name="z_late", tag=bank)
            else:
                z[t, i, half] = psum.tile([P, BANK], F32, name="z%d" % t, bufs=E_BANKS if t == HEAD_E else 1)
            if turned:
                for c in range(4):
                    cols = slice(BANK * half + P * c, BANK * half + P * (c + 1))
                    nc.tensor.matmul_mx(
                        out=z[t, i, half][:, P * c:P * (c + 1)],
                        lhsT=wh_q[:, t, cols].bitcast(FP8X4),
                        lhsT_scale=wh_s[:, t, cols],
                        rhs=h_q[:, i, :].bitcast(FP8X4),
                        rhs_scale=h_s[:, i, :],
                        start=True,
                        stop=True,
                    )
            else:
                nc.tensor.matmul_mx(
                    out=z[t, i, half][:],
                    lhsT=h_q[:, i, :].bitcast(FP8X4),
                    lhsT_scale=h_s[:, i, :],
                    rhs=wh_q[:, t, half_cols(half)].bitcast(FP8X4),
                    rhs_scale=wh_s[:, t, half_cols(half)],
                    start=True,
                    stop=True,
                )

        def exp_z0(i, half):
            if half == 0:
                inv_p[i] = work.tile([P, N], F32, name="ee")
            nc.scalar.activation(out=inv_p[i][:, half_cols(half)], in_=z[HEAD_P, i, half][:], func=ACT.Exp, scale=-1.0)

        def tanh_z1(i, half):
            z1_tanh[i, half] = work.tile([P, BANK], F32, name="tt")
            nc.scalar.activation(out=z1_tanh[i, half][:], in_=z[HEAD_ERR, i, half][:], func=ACT.Tanh, scale=0.5)

        def diff_matmul(i, half):
            diff[i, half] = psum.tile([P, BANK], F32, name="up")
            nc.tensor.matmul(out=diff[i, half][:], lhsT=neg2[:], rhs=y_sb[i][:, half_cols(half)], start=True, stop=False)
            for c in range(4):
                cols = slice(P * c, P * (c + 1))
                nc.tensor.matmul(
                    out=diff[i, half][:, cols],
                    lhsT=z1_tanh[i, half][:, cols],
                    rhs=ident[:],
                    is_transpose=True,
                    start=False,
                    stop=(c == 3),
                )

        def add_turned(bank, src, start, stop):
            for c in range(4):
                cols = slice(P * c, P * (c + 1))
                nc.tensor.matmul(
                    out=bank[:, cols], lhsT=src[:, cols], rhs=ident[:], is_transpose=True,
                    start=(start and c == 0), stop=(stop and c == 3),
                )

        def diff_turned(i, half):
            diff[i, half] = psum.tile([P, BANK], F32, name="up")
            for c in range(4):
                cols = slice(BANK * half + P * c, BANK * half + P * (c + 1))
                nc.tensor.matmul(
                    out=diff[i, half][:, P * c:P * (c + 1)], lhsT=y_sb[i][:, cols], rhs=neg2[:], start=(c == 0), stop=False
                )
            add_turned(diff[i, half], z1_tanh[i, half], False, True)

        def minus_e(i, half):
            neg_e[i, half] = work.tile([P, BANK], F32, name="tt")
            nc.scalar.activation(out=neg_e[i, half][:], in_=z[HEAD_E, i, half][:], func=ACT.Copy, scale=-1.0)

        def gap_matmul(i, half, bank):
            gap_ps[i, half] = psum.tile([P, BANK], F32, name="gap_ps", tag=bank)
            add_turned(gap_ps[i, half], neg_e[i, half], True, False)
            add_turned(gap_ps[i, half], err[i, half], False, True)

        def weigh_gap_from_psum(i, half):
            cols = half_cols(half)
            nc.vector.tensor_tensor(out=gap[i][:, cols], in0=weight[i][:, cols], in1=gap_ps[i, half][:], op=ALU.mult)

        def square(i, half):
            err[i, half] = work.tile([P, BANK], F32, name="er", bufs=4)
            nc.scalar.activation(out=err[i, half][:], in_=diff[i, half][:], func=ACT.Square, scale=0.5, bias=0.5)

        def clamp(i):
            nc.vector.tensor_scalar(out=inv_p[i][:], in0=inv_p[i][:], scalar1=4.0, scalar2=1.0, op0=ALU.min, op1=ALU.add)

        def gpsimd_cols(i):
            return N - {0: FIRST_REST, TILES - 1: LAST_REST}.get(i, 0)

        def weight_on_gpsimd(i):
            weight[i] = work.tile([P, N], F32, name="ww", bufs=TILES)
            cols = slice(0, gpsimd_cols(i))
            nc.gpsimd.tensor_tensor(out=weight[i][:, cols], in0=inv_p[i][:, cols], in1=o_sb[i][:, cols], op=ALU.mult)

        def weight_rest(i):
            if gpsimd_cols(i) < N:
                cols = slice(gpsimd_cols(i), N)
                nc.vector.tensor_tensor(out=weight[i][:, cols], in0=inv_p[i][:, cols], in1=o_sb[i][:, cols], op=ALU.mult)

        def err_minus_e(i, half):
            if half == 0:
                gap[i] = work.tile([P, N], F32, name="ff", bufs=2)
            nc.vector.tensor_tensor(out=gap[i][:, half_cols(half)], in0=err[i, half][:], in1=z[HEAD_E, i, half][:], op=ALU.subtract)

        def weigh_gap(i, cols):
            nc.vector.tensor_tensor(out=gap[i][:, cols], in0=weight[i][:, cols], in1=gap[i][:, cols], op=ALU.mult)

        def sum_and_store(i, c0, width):
            half, cols = c0 // BANK, slice(c0, c0 + width)
            e = z[HEAD_E, i, half][:, c0 - BANK * half:c0 - BANK * half + width]
            nc.vector.tensor_tensor(out=weight[i][:, cols], in0=e, in1=gap[i][:, cols], op=ALU.add)
            nc.sync.dma_start(out=out[P * i:P * (i + 1), cols], in_=weight[i][:, cols])

        nc.tensor.matmul(
            out=gain_ps[:], lhsT=ident_bf[:], rhs=gain[:].unsqueeze(1).to_broadcast([P, P, 4]), start=True, stop=True
        )
        widen_on_vector(HEAD_P,0,LO)
        widen_on_scalar(HEAD_P,1,LO)
        widen_on_vector(HEAD_P,0,HI)
        widen_on_vector(HEAD_P,2,LO)
        widen_on_scalar(HEAD_P,3,LO)
        widen_on_vector(HEAD_P,2,HI)
        wh_turn(0)
        wh_turn(1)
        widen_on_vector(HEAD_ERR,0,LO)
        widen_on_vector(HEAD_P,1,HI)
        widen_on_scalar(HEAD_ERR,1,LO)
        widen_on_vector(HEAD_ERR,2,LO)
        widen_on_scalar(HEAD_ERR,3,LO)
        widen_on_vector(HEAD_P,3,HI)
        widen_on_vector(HEAD_ERR,0,HI)
        wh_interleave(HEAD_ERR,LO)
        w_interleave(0)
        w_interleave(1)
        widen_on_scalar(HEAD_ERR,1,HI)
        widen_on_scalar(HEAD_ERR,2,HI)
        wh_copy(0)
        widen_on_scalar(HEAD_ERR,3,HI)
        x_transpose(0)
        wh_turn(2)
        x_transpose(1)
        wh_turn(3)
        wh_copy(1)
        x_copy(0)
        x_quantize(0)
        w_quantize()
        widen_on_scalar(HEAD_E,0,LO)
        widen_on_scalar(HEAD_E,1,LO)
        wh_copy(2)
        x_copy(1)
        widen_on_scalar(HEAD_E,2,LO)
        widen_on_scalar(HEAD_E,3,LO)
        wh_copy(3)
        h_matmul(0)
        h_activate(0)
        x_transpose(2)
        widen_on_scalar(HEAD_E,0,HI)
        x_copy(2)
        wh_interleave(HEAD_ERR,HI)
        x_quantize(1)
        h_matmul(1)
        x_transpose(3)
        x_transpose(4)
        wh_quantize(HEAD_ERR,LO)
        wh_quantize(HEAD_P,LO)
        h_gain(0)
        wh_quantize(HEAD_P,HI)
        h_quantize(0)
        h_activate(1)
        widen_on_scalar(HEAD_E,1,HI)
        widen_on_scalar(HEAD_E,2,HI)
        z_matmul(HEAD_P, 0,0)
        z_matmul(HEAD_ERR, 0,0)
        wh_quantize(HEAD_ERR,HI)

        for k in range(TILES - 3):
            exp_z0(k, 0)
            if k > 1:
                x_transpose(k + 3)
            if k > 1:
                sum_and_store(k - 2, 0, BANK)
            if 0 < k <= 1:
                square(k - 1, 1)
            tanh_z1(k, 0)
            z_matmul(HEAD_P, k, 1)
            if k > 1:
                z_matmul(HEAD_E, k - 1, 1)
            if k > 1:
                square(k - 1, 1)
            if k == 0:
                widen_on_scalar(HEAD_E, 3, HI)
            z_matmul(HEAD_ERR, k, 1)
            if k > 1:
                sum_and_store(k - 2, BANK, BANK)
            if k != 1:
                h_gain(k + 1)
            if k == 0:
                wh_interleave(HEAD_E, LO)
            x_copy(k + 3)
            if k > 1:
                z_matmul(HEAD_E, k, 0)
            diff_matmul(k, 0)
            if k == 1:
                z_matmul(HEAD_E, k, 0)
            exp_z0(k, 1)
            if k > 0:
                err_minus_e(k - 1, 1)
            if k > 0:
                h_matmul(k + 2)
            tanh_z1(k, 1)
            if k > 0:
                weight_rest(k - 1)
            h_quantize(k + 1)
            if k == 0:
                x_quantize(2)
                h_matmul(2)
                wh_quantize(HEAD_E, LO)
                wh_interleave(HEAD_E, HI)
            x_quantize(k + 3)
            z_matmul(HEAD_P, k + 1, 0)
            square(k, 0)
            z_matmul(HEAD_ERR, k + 1, 0)
            if 0 < k <= 0:
                weigh_gap(k - 1, BOTH)
            clamp(k)
            weight_on_gpsimd(k)
            if k > 0:
                weigh_gap(k - 1, BOTH)
            h_activate(k + 2)
            if k == 0:
                z_matmul(HEAD_E, 0, 0)
            diff_matmul(k, 1)
            if k == 0:
                wh_quantize(HEAD_E, HI)
                z_matmul(HEAD_E, 0, 1)
            err_minus_e(k, 0)
            if k == 0:
                h_gain(2)

        h_matmul(7)
        exp_z0(5,0)
        sum_and_store(3, 0, BANK)
        tanh_z1(5,0)
        z_matmul(HEAD_P, 5,1)
        z_matmul(HEAD_ERR, 5,1,None,False)
        z_matmul(HEAD_E, 4,1)
        square(4,1)
        sum_and_store(3, BANK, BANK)
        h_gain(6)
        diff_matmul(5,0)
        h_activate(7)
        exp_z0(5,1)
        err_minus_e(4,1)
        tanh_z1(5,1)
        z_matmul(HEAD_E, 5,1,"aux",True)
        h_quantize(6)
        z_matmul(HEAD_P, 6,0)
        z_matmul(HEAD_E, 5,0)
        square(5,0)
        z_matmul(HEAD_ERR, 6,0)
        diff_turned(5,1)
        clamp(5)
        weight_on_gpsimd(5)
        weigh_gap(4,BOTH)
        minus_e(5,1)
        err_minus_e(5,0)
        exp_z0(6,0)
        sum_and_store(4, 0, BANK)
        tanh_z1(6,0)
        z_matmul(HEAD_P, 6,1)
        square(5,1)
        z_matmul(HEAD_ERR, 6,1)
        z_matmul(HEAD_E, 6,0)
        h_gain(7)
        sum_and_store(4, BANK, BANK)
        diff_matmul(6,0)
        gap_matmul(5,1,"g_ps")
        exp_z0(6,1)
        tanh_z1(6,1)
        h_quantize(7)
        z_matmul(HEAD_P, 7,0)
        square(6,0)
        z_matmul(HEAD_ERR, 7,0)
        diff_matmul(6,1)
        z_matmul(HEAD_E, 5,1)
        clamp(6)
        weight_on_gpsimd(6)
        weigh_gap(5,LO)
        err_minus_e(6,0)
        exp_z0(7,0)
        weigh_gap_from_psum(5,1)
        sum_and_store(5, 0, BANK)
        tanh_z1(7,0)
        z_matmul(HEAD_P, 7,1)
        z_matmul(HEAD_E, 6,1,"aux")
        square(6,1)
        z_matmul(HEAD_ERR, 7,1)
        diff_matmul(7,0)
        sum_and_store(5, BANK, BANK)
        z_matmul(HEAD_E, 7,0)
        exp_z0(7,1)
        err_minus_e(6,1)
        tanh_z1(7,1)
        square(7,0)
        clamp(7)
        weight_on_gpsimd(7)
        weigh_gap(6,BOTH)
        diff_matmul(7,1)
        err_minus_e(7,0)
        z_matmul(HEAD_E, 7,1,"g_ps")
        sum_and_store(6, 0, BANK)
        square(7,1)
        sum_and_store(6, BANK, BANK)
        err_minus_e(7,1)
        weight_rest(7)
        weigh_gap(7,LO)
        weigh_gap(7,slice(BANK,N-LAST_STORE))
        sum_and_store(7, 0, BANK)
        weigh_gap(7,slice(N-LAST_STORE,N))
        sum_and_store(7,BANK,BANK-LAST_STORE)
        sum_and_store(7,N-LAST_STORE,LAST_STORE)
